import numpy as np, ml_dtypes
CORES = [3,7,11,15,131,135,139,143]
N = 8
BF = ml_dtypes.bfloat16
def f(rng, *shape):
    return (rng.standard_normal(shape, dtype=np.float32) * np.exp2(rng.integers(-2, 3, shape[:-1] + (1,)))).astype(BF)
def wide(rng, *shape):
    v = f(rng, *shape).astype(np.float32); k = shape[:-2] + (1, shape[-1])
    return (v * np.exp2(rng.integers(-6, 7, k)) * (rng.random(k) > 0.0625)).astype(BF)
P, F, M, C, T, K, D = 2048, 384, 10, 1024, 4, 48, 6
def parts(rng):
    pic = rng.standard_normal((N, 8, 1, P), dtype=np.float32) + rng.standard_normal((N, 8, 16, P), dtype=np.float32)
    pic = (pic * np.exp2(rng.integers(-2, 3, (N, 8, 16, 1)))).astype(np.float32)
    s = rng.integers(0, P, (N, 8, 16, F)); o = rng.integers(0, P, (N, 8, 16, T)); th = M // 2 + rng.integers(-1, 2, (N, 8, T))
    return pic, s, o, th, rng.integers(-256, 257, (N, 8, 16, C)), rng.integers(0, P, (N, 8, 16, C))
def pack(pic, s, o, th, b, e):
    return {"pic": pic.reshape(N, 128, P).astype(BF), "shp": s.reshape(N, 128, F).astype(np.int32), "ofs": o.reshape(N, 128, T).astype(np.int32),
            "thr": th.astype(np.int32), "inc": b.reshape(N, 128, C).astype(np.float32).astype(BF), "ex": e.reshape(N, 128, C).astype(np.int32)}
def setup_inputs(rng):
    return pack(*parts(rng))
def setup_inputs_edge(rng):
    pic, s, o, th, b, e = parts(rng)
    lv = np.array([0, 3, 4, 8, 9, 11, 12, 16])[rng.integers(0, 8, (N, 8, 1, P))]; ch = np.argsort(rng.random((N, 8, 16, 1)), axis=2)
    pic = (ch < lv).astype(np.float32) * np.exp2(rng.integers(-2, 3, (N, 8, 16, 1)))
    return pack(pic, s, o, 3 * M // 4 + rng.integers(-1, 2, (N, 8, T)), b, e)
def setup_inputs_ends(rng):
    pic, s, o, th, b, e = parts(rng)
    s = rng.choice(np.array([0, 1, P // 2, P - 1]), s.shape); o = rng.choice(np.array([0, 1, P - 1]), o.shape)
    b = rng.choice(np.array([-256, -255, -2, -1, 0, 1, 255, 256]), b.shape); e[:, ::2] = rng.choice(np.array([0, 1, P - 1]), (N, 4, 16, C))
    th[:, :3] = 0; th[:, 3] = 16
    pic[:, 4] = -(np.arange(P) >> 5)
    x = np.arange(16)[:, None] * (P >> 4) + rng.integers(0, P >> 5, (N, 16, F))
    s[:, 4] = np.where(rng.random((N, 1, F)) < 0.5, P - 1 - x, x); o[:, 4, :, 0] = 0; th[:, 4, 0] = M
    return pack(pic, s, o, th, b, e)
def setup_inputs_mixed(rng):
    pic, s, o, th, b, e = parts(rng)
    x = np.arange(P); ch = np.argsort(rng.random((N, 3, 16, 1)), axis=2) < 10
    pic[:, :3] = np.where(ch | ((x & 1) == 0), -(x >> 5), x >> 5) * np.exp2(rng.integers(-2, 3, (N, 3, 16, 1)))
    code = rng.integers(0, C - 1, (N, 3, F)); odd = rng.integers(0, 2, (N, 3, F))
    code[:, 0, :K] = np.argsort(rng.random((N, C)), axis=1)[:, :K]; odd[:, 0, :K] = 0
    code[:, 1:, ::3] = C - 1; odd[:, 1, 0] = 0; odd[:, 1, 3] = 1; odd[:, 2, ::3] = 1; odd[:, 2, 1] = 0
    lv = np.zeros((N, 3, 16, F), np.int64)
    for m in range(M):
        lv[:, :, m + D] = lv[:, :, m] + 2 * ((code >> m) & 1) - 1
    at = (8 + lv) * (P >> 4) + rng.integers(0, P >> 5, lv.shape); at = at - (at & 1) + odd[:, :, None, :]
    s[:, :3] = (at - o[:, :3, :, :1]) & (P - 1)
    pic[:, 3] = rng.standard_normal((N, 16, P), dtype=np.float32)
    pic[:, 4:6] = 3 * rng.standard_normal((N, 2, 1, P), dtype=np.float32) + rng.standard_normal((N, 2, 16, P), dtype=np.float32)
    for g, w in enumerate(([M, 16, 0, 1], [1, 0, 0, 0], [1, 16, 0, M], [1, 1, 0, 1], [M, M - 1, 16, 0], [M - 1, 0, M, 16], [M // 2, 16, 0, M // 2], [13, 0, 14, 15])):
        th[:, g] = np.resize(np.array(w), T)
    return pack(pic, s, o, th, b, e)
def setup_inputs_repeat(rng):
    pic, s, o, th, b, e = parts(rng)
    s[:, ::2] = s[:, ::2][..., rng.integers(0, 5, F)]; th[:, ::2] = 0
    s[:, 6, :, :T * K] = rng.integers(0, P, (N, 16, T * K))
    pic[:, 2:4] = 1.0; th[:, 2] = M; th[:, 3] = M + 1
    return pack(pic, s, o, th, b, e)
def setup_inputs_spread(rng):
    pic, s, o, th, b, e = parts(rng); lp = P.bit_length() - 1
    w = wide(rng, N, 128, P).astype(np.float32).reshape(N, 8, 16, P)
    pic = np.where(rng.random((N, 8, 1, P)) < 0.5, np.abs(w), w) * np.exp2(rng.integers(-60, 61, (N, 8, 16, 1)))
    pic = np.where(np.abs(pic) < 2.0 ** -78, 0.0, pic)
    s = np.minimum(np.exp2(lp * rng.random(s.shape)).astype(np.int64), P - 1); e = np.minimum(np.exp2(lp * rng.random(e.shape)).astype(np.int64), P - 1)
    b = np.minimum(np.exp2(8 * rng.random(b.shape)).astype(np.int64), 256) * rng.integers(-1, 2, b.shape)
    return pack(pic, s, o, rng.integers(2, M - 1, (N, 8, T)), b, e)
def check_inputs(d):
    bad = []
    for k, lo, hi in (("shp", 0, P - 1), ("ofs", 0, P - 1), ("thr", 0, 16), ("ex", 0, P - 1)):
        if np.min(d[k]) < lo or np.max(d[k]) > hi: bad.append("range of " + k)
    p = np.abs(np.asarray(d["pic"]).astype(np.float32))
    if not np.all((p == 0) | ((p >= 2.0 ** -100) & (p <= 2.0 ** 100))): bad.append("sizes of pic")
    a = np.asarray(d["inc"]).astype(np.float32)
    if not (np.all(np.abs(a) <= 256) and np.all(a == np.floor(a))): bad.append("whole numbers of inc")
    return bad
def reference(pic, shp, ofs, thr, inc, ex):
    im = pic.astype(np.float32).reshape(N, 8, 16, P); s = shp.astype(np.int64).reshape(N, 8, 16, F); o = ofs.astype(np.int64).reshape(N, 8, 16, T)
    b = inc.astype(np.float32).astype(np.int64).reshape(N, 8, 16, C); e = ex.astype(np.int64).reshape(N, 8, 16, C); bit = 2 ** np.arange(M)[:, None]
    for t in range(T):
        d = D - t; after = np.array(b); new = []
        for r in range(N):
            q = (r + 1 + t) % N
            x = (s[r] + o[r, :, :, t:t + 1]) & (P - 1)
            v = np.take_along_axis(im[r], x.reshape(8, 1, 16 * F), 2).reshape(8, 16, 16, F)
            n = np.add.reduce((v[:, :, :M] > v[:, :, d:d + M]).astype(np.int64), axis=1)
            code = np.add.reduce((n >= 9) * bit, axis=1)
            sure = np.add.reduce(((n >= 12) | (n <= 3)).astype(np.int64), axis=1) >= thr[r][:, t:t + 1]
            up = np.take_along_axis(b[q], code[:, None, :], 2); like = np.take_along_axis(e[q], code[:, None, :], 2)
            new.append(np.where(sure[:, None, :], (s[r] + up) & (P - 1), like))
            used = np.zeros((8, C + 1), bool)
            np.put_along_axis(used, np.where(sure, code, C)[:, t * K:t * K + K], True, 1)
            after[q] = np.where(used[:, None, :C], b[q] >> 1, b[q])
        s = np.stack(new); b = after
    return {"ys": s.reshape(N, 128, F).astype(np.float32), "yi": b.reshape(N, 128, C).astype(np.float32).astype(BF)}

@@ -1,0 +1,560 @@
+from concourse.bass import DstId, RemoteDMATransfer
+from concourse.mybir import AluOpType, ActivationFunctionType
+
+ALU = AluOpType
+ACT = ActivationFunctionType
+
+P, F, C, NT, KH, D0 = 2048, 384, 1024, 4, 48, 6
+WL = 3
+FB = 64 * WL
+NB = F // FB
+W = 16 * WL
+B = 4 * WL
+MV = 40 * WL
+HV = 2
+SPLIT = (("B",), ("A1", "C", "A2"))
+HEAD = 768
+PW = 2 * P + 2 * HEAD
+IH = 64
+IW = IH + C
+MW = 136
+RAW = 897
+SEG = 65
+
+SETS = []
+for _t in range(NT):
+    _d = D0 - _t
+    _x = 5 if _d == 3 else 2
+    _m = [_b0 + _x * (_k >> 1) + (_k & 1) for _b0 in (0, _d) for _k in range(4)]
+    _rest = sorted(set(range(10)) - set(_m))
+    SETS.append({"B": (_d, _x), "A1": (0, _x), "A2": (2 * _d, _x), "C": (_rest[0], _rest[1] - _rest[0], _d), "m": _m + _rest})
+MASTERS = []
+for _t in range(NT):
+    for _n in ("B", "C", "A1", "A2"):
+        if SETS[_t][_n] not in MASTERS:
+            MASTERS.append(SETS[_t][_n])
+NM = len(MASTERS)
+
+SCRATCH = {
+    "picw": ("sbuf", [128, PW], "bfloat16"),
+    "exo": ("sbuf", [128, C], "int32"),
+    "inco": ("sbuf", [128, C], "bfloat16"),
+    "ofi": ("sbuf", [128, 4], "int32"),
+    "off": ("sbuf", [128, 4], "float32"),
+    "thi": ("sbuf", [128, 4], "int32"),
+    "thb": ("sbuf", [128, 4], "bfloat16"),
+    "bth": ("sbuf", [128, 4], "float32"),
+    "ob": ("sbuf", [128, 3 * W], "float16"),
+    "ta": ("sbuf", [128, F], "int32"),
+    "tb": ("sbuf", [128, F], "int32"),
+    "ysf": ("sbuf", [128, F], "float32"),
+    "mst": ("sbuf", [128, NM * MW], "bfloat16"),
+    "ones": ("sbuf", [128, 128], "bfloat16"),
+    "zer": ("sbuf", [128, 4 * W], "bfloat16"),
+    "idn": ("sbuf", [128, 13 * 128], "bfloat16"),
+    "bo": ("sbuf", [128, 8], "bfloat16"),
+    "bo1": ("sbuf", [128, 8], "bfloat16"),
+    "bot": ("sbuf", [128, 128], "bfloat16"),
+    "hot": ("sbuf", [128, 10 * B], "bfloat16"),
+    "wgt": ("sbuf", [128, 5 * B], "bfloat16"),
+    "tbi": ("sbuf", [128, 4], "float32"),
+    "tiny": ("sbuf", [128, 4], "float32"),
+    "pi": ("sbuf", [128, 4], "int32"),
+    "pa": ("sbuf", [128, 4], "int32"),
+    "af": ("sbuf", [128, 4], "float32"),
+    "l2": ("sbuf", [128, F // 16], "float32"),
+    "low": ("sbuf", [128, NB * 2 * B], "float32"),
+    "lo3": ("sbuf", [128, 4], "float32"),
+    "kr": ("sbuf", [128, SEG], "float32"),
+    "cst": ("sbuf", [128, 3 * SEG], "float32"),
+    "eq": ("sbuf", [128, 3 * SEG], "float32"),
+    "sc": ("sbuf", [128, 3 * SEG], "float32"),
+    "io2": ("sbuf", [128, IW], "float32"),
+    "slo": ("sbuf", [128, NT * 2 * KH], "uint16"),
+    "pc": ("psum", [128, 512], "float32"),
+    "pz": ("psum", [128, 512], "float32"),
+}
+for _t in range(NT):
+    SCRATCH["w2_%d" % _t] = ("sbuf", [128, F + C], "int32")
+    SCRATCH["sli%d" % _t] = ("sbuf", [128, 2 * KH], "uint16")
+    SCRATCH["hvo%d" % _t] = ("sbuf", [128, KH], "int32")
+    SCRATCH["hvi%d" % _t] = ("sbuf", [128, KH], "int32")
+for _t in range(NT + 1):
+    SCRATCH["inc%d" % _t] = ("sbuf", [128, IW], "bfloat16")
+for _j in range(NB):
+    SCRATCH["xh%d" % _j] = ("sbuf", [128, FB], "float16")
+    SCRATCH["lst%d" % _j] = ("sbuf", [128, 4 * W], "uint16")
+    SCRATCH["gb%d" % _j] = ("sbuf", [128, 16 * W], "bfloat16")
+    SCRATCH["gx%d" % _j] = ("sbuf", [128, 16 * W], "bfloat16")
+    SCRATCH["cmp%d" % _j] = ("sbuf", [128, 32 * W], "bfloat16")
+    SCRATCH["cmc%d" % _j] = ("sbuf", [128, 8 * W], "bfloat16")
+    SCRATCH["pln%d" % _j] = ("sbuf", [128, 3 * 128], "bfloat16")
+    SCRATCH["sg%d" % _j] = ("sbuf", [128, B], "bfloat16")
+    SCRATCH["yr%d" % _j] = ("sbuf", [128, 2 * B], "float32")
+    SCRATCH["idx%d" % _j] = ("sbuf", [128, 2 * B], "uint16")
+    SCRATCH["ga%d" % _j] = ("sbuf", [128, FB], "float32")
+for _j in range(2):
+    SCRATCH["pl%d_0" % _j] = ("psum", [128, 512], "float32")
+    SCRATCH["pl%d_1" % _j] = ("psum", [128, 512], "float32")
+    SCRATCH["pv%d" % _j] = ("psum", [128, 512], "float32")
+
+SEMAPHORES = (["qv", "qs", "qp", "qg", "sent"] + ["d%d" % i for i in range(16)] + ["ae%d" % t for t in range(NT)]
+              + ["ai%d" % t for t in range(NT + 1)] + ["au%d" % t for t in range(NT)])
+
+CYC, FIX, GAT, SCA, PEC, HOP = 0.00104, 0.07, 1.56, 3.8, 0.0006, 0.08
+T_BANK0, T_UPD, T_FWD = 7.5, 4.0, 6.0
+LOOK = 0.05
+ORDER = [3, 71, 0, 4, 10, 1, 2, 5, 6, 7, 8, 9, 32, 61, 11, 12, 13, 62, 94, 57, 67, 95, 96, 70, 97, 99, 98, 15, 45, 14, 48, 50, 21, 89, 49,
+         17, 16, 1000, 43, 39, 34, 37, 33, 40, 35, 41, 36, 38, 44, 42, 72, 100, 18, 1001, 1002, 77, 30, 24, 47, 1003, 20, 87, 80, 46, 76,
+         74, 1004, 22, 26, 28, 19, 79, 25, 88, 78, 75, 51, 105, 106, 63, 101, 59, 58, 68, 109, 102, 110, 52, 107, 64, 60, 103, 108, 104,
+         113, 53, 129, 131, 130, 112, 65, 73, 114, 66, 111, 116, 133, 117, 54, 132, 115, 137, 136, 134, 135, 139, 138, 118, 119, 55, 120,
+         140, 122, 56, 82, 121, 124, 171, 141, 123, 125, 142, 126, 143, 144, 174, 81, 83, 127, 128, 153, 154, 156, 157, 155, 147, 145,
+         146, 148, 172, 84, 86, 85, 173, 162, 160, 161, 158, 175, 159, 163, 164, 176, 177, 180, 149, 200, 197, 150, 69, 181, 151, 152,
+         1005, 1006, 1020, 23, 90, 92, 1007, 91, 179, 178, 183, 182, 184, 185, 165, 241, 186, 187, 188, 166, 168, 167, 169, 198, 199,
+         190, 189, 191, 192, 193, 194, 170, 195, 196, 201, 203, 228, 223, 202, 230, 232, 204, 205, 231, 224, 227, 225, 226, 244, 242,
+         245, 207, 243, 229, 208, 246, 247, 233, 206, 234, 209, 250, 251, 210, 270, 211, 212, 267, 213, 249, 254, 214, 248, 255, 256,
+         31, 27, 1030, 29, 1011, 1021, 1031, 93, 216, 215, 217, 253, 252, 218, 257, 219, 220, 221, 222, 235, 236, 237, 239, 238, 240,
+         258, 311, 259, 260, 261, 262, 263, 264, 265, 298, 266, 293, 268, 269, 271, 294, 272, 295, 296, 297, 273, 276, 274, 278, 314,
+         337, 312, 315, 313, 277, 316, 275, 301, 318, 280, 317, 281, 340, 279, 323, 282, 283, 284, 319, 302, 300, 321, 299, 320, 303,
+         304, 286, 285, 324, 287, 288, 289, 290, 325, 322, 326, 327, 328, 1012, 1022, 291, 292, 305, 306, 309, 308, 307, 338, 339, 329,
+         330, 331, 343, 332, 341, 333, 344, 334, 342, 347, 335, 336, 310, 346, 348, 345, 368, 370, 372, 371, 363, 373, 374, 369, 349,
+         364, 365, 366, 350, 351, 352, 353, 354, 356, 355, 358, 357, 359, 360, 361, 362, 375, 376, 377, 1013, 1023, 380, 367, 381, 378,
+         379]
+INFO = {}
+
+
+def list_order(nodes):
+    n = len(nodes)
+    succ = [[] for _ in range(n)]
+    left = [0] * n
+    for i, nd in enumerate(nodes):
+        for p, lat in nd["pre"]:
+            succ[p].append((i, lat))
+            left[i] += 1
+    prio = [0.0] * n
+    for i in range(n - 1, -1, -1):
+        prio[i] = nodes[i]["cost"] + nodes[i]["lat"] + max([prio[s] + lat for s, lat in succ[i]] + [0.0])
+    ready = [0.0] * n
+    free, order, cand = {}, [], [i for i in range(n) if left[i] == 0]
+    while cand:
+        first = min(cand, key=lambda i: (max(ready[i], free.get(nodes[i]["eng"], 0.0)), -prio[i], i))
+        e = nodes[first]["eng"]
+        t = max(ready[first], free.get(e, 0.0))
+        pick = max([i for i in cand if nodes[i]["eng"] == e and ready[i] <= t + LOOK], key=lambda i: (prio[i], -i))
+        t = max(t, ready[pick])
+        cand.remove(pick)
+        free[e] = t + nodes[pick]["cost"]
+        order.append(pick)
+        for s, lat in succ[pick]:
+            ready[s] = max(ready[s], free[e] + nodes[pick]["lat"] + lat)
+            left[s] -= 1
+            if left[s] == 0:
+                cand.append(s)
+    return order
+
+
+def call_order(nodes):
+    pos = {k: i for i, k in enumerate(ORDER)}
+    if all(nd["key"] in pos for nd in nodes) and all(pos[nodes[p]["key"]] < pos[nd["key"]] for nd in nodes for p, _ in nd["pre"]):
+        return sorted(range(len(nodes)), key=lambda i: pos[nodes[i]["key"]])
+    return list_order(nodes)
+
+
+def rank_program(g, core, T, topo):
+    rank = T.rank_of(core)
+    if rank is None:
+        return
+    cores = list(T.cores)
+    N = len(cores)
+    Q = {"g": g, "v": g.vector, "s": g.scalar, "p": g.tensor, "y": g.sync}
+    QSEM = {"g": "qg", "v": "qv", "s": "qs", "p": "qp"}
+    nodes, last_w, readers = [], {}, {}
+    ndma, nkey = [0], [0]
+    totals = {}
+
+    def add(eng, fn, cost, reads=(), writes=(), ext=(), after=(), lat=0.0, kind="c", name="", cm=None, role=None):
+        i = len(nodes)
+        dep = set()
+        for k in reads:
+            if k in last_w:
+                dep.add(last_w[k])
+        for k in writes:
+            if k in last_w:
+                dep.add(last_w[k])
+            dep.update(readers.get(k, []))
+        for k in reads:
+            readers.setdefault(k, []).append(i)
+        for k in writes:
+            last_w[k] = i
+            readers[k] = []
+        dep.discard(i)
+        nd = {"eng": eng, "fn": fn, "cost": cost, "dep": sorted(dep), "ext": list(ext), "lat": lat, "kind": kind,
+              "pre": [(p, HOP) for p in sorted(dep)] + list(after), "name": name, "cm": cm}
+        if kind == "d":
+            nd["sem"] = "d%d" % ndma[0]
+            ndma[0] += 1
+        if role is None:
+            nd["key"] = nkey[0]
+            nkey[0] += 1
+        else:
+            nd["key"] = 1000 + role
+        nodes.append(nd)
+        return i
+
+    def vec(fn, n, reads, writes, c=1.0, **kw):
+        return add("v", lambda q: [fn(q)], FIX + max(n * c, 32) * CYC, reads, writes, cm=(n, c), **kw)
+
+    def act(out, in_, func, n, reads, writes, c=1.0, bias=0.0, scale=1.0, **kw):
+        return add("s", lambda q: [q.activation(out, in_, func, bias=bias, scale=scale)], FIX + max(n * c, 32) * CYC, reads, writes,
+                   cm=(n, c), **kw)
+
+    def mm(lst, reads, writes, **kw):
+        cyc = sum(max(64, x[5]) if x[5] > 0 else -x[5] for x in lst)
+        return add("p", lambda q: [q.matmul(o, l, r, a, b) for o, l, r, a, b, _ in lst], cyc * PEC + 0.1, reads, writes, cm=cyc, **kw)
+
+    def gps(fn, n, reads, writes, **kw):
+        return add("g", lambda q: [fn(q)], 0.2 + 2 * n * CYC, reads, writes, **kw)
+
+    def dma(eng, out, in_, lat, reads, writes, **kw):
+        return add(eng, lambda q: [q.dma_start(out, in_)], 0.1, reads, writes, lat=lat, kind="d", **kw)
+
+    def ts(out, in0, s1, s2, op0, op1=None):
+        if op1 is None:
+            return lambda q: q.tensor_scalar(out, in0, s1, None, op0)
+        return lambda q: q.tensor_scalar(out, in0, s1, s2, op0, op1)
+
+    def fill(out, n, value):
+        return lambda q: q.iota(out, [[0, n]], value, 0, allow_small_or_imprecise_dtypes=True)
+
+    def same_chip(a, b):
+        return b in topo.cores_of(a)
+
+    def far_mask(a):
+        return [topo.mask(a, b) for b in cores if not same_chip(a, b)][0]
+
+    def engines(a, b):
+        if same_chip(a, b):
+            return [e for e in topo.engines(a, b) if not far_mask(a) >> e & 1]
+        return list(topo.engines(a, b))
+
+    def bits(es):
+        return sum(1 << e for e in es)
+
+    def handed_on(r, t):
+        return t >= 1 and same_chip(cores[r], cores[(r + 1) % N])
+
+    def src_ex(r, t):
+        return (r + 1) % N if handed_on(r, t) else (r + 1 + t) % N
+
+    def src_inc(r, t):
+        return src_ex(r, t) if t <= 1 else ((r + 1) % N if t < NT else (r - NT) % N)
+
+    def src_upd(r, t):
+        return (r + 1) % N if t < NT - 1 else (r - NT) % N
+
+    def arr_ex(t):
+        return ("ae%d" % t, (2 if t == 0 else 1) * len(engines(cores[src_ex(rank, t)], core)))
+
+    def arr_inc(t):
+        return ("ai%d" % t, len(engines(cores[src_inc(rank, t)], core)))
+
+    def arr_upd(t):
+        return ("au%d" % t, len(engines(cores[src_upd(rank, t)], core)))
+
+    chain = []
+
+    def send(role, r, out, in_, sem, reads, ext=(), after=()):
+        es = engines(core, cores[r])
+        rid, pid = topo.addr(cores[r], core)
+        totals["sent"] = totals.get("sent", 0) + len(es)
+        i = add("g", lambda q: [q.remote_dma(out, in_, T.sem[sem], T.sem.sent, pid, rid, bits(es))], 0.5, reads, (), ext=ext,
+                after=[(c, 0.0) for c in chain[-1:]] + list(after), kind="r", role=role, name="r%d" % role)
+        chain.append(i)
+        return i
+
+    def slo(t, n):
+        return T.slo[:, 2 * KH * t:2 * KH * t + n]
+
+    def send_update(role, r, t):
+        es = engines(core, cores[r])
+        rid, pid = topo.addr(cores[r], core)
+        h = len(es) // 2
+        totals["sent"] = totals.get("sent", 0) + len(es)
+        tr = [RemoteDMATransfer(dst_ids=[DstId(rid=rid, pnc=pid)], dma_engine_mask=bits(e), remote_sem=T.sem["au%d" % t], src=a, dst=b)
+              for e, a, b in ((es[:h], slo(t, 2 * KH), T["sli%d" % t][:]), (es[h:], T["hvo%d" % t][:], T["hvi%d" % t][:]))]
+        i = add("g", lambda q: [q.remote_dma_fused(tr, local_sem=T.sem.sent)], 0.5, ["slo%d" % t, "hvo%d" % t], (),
+                after=[(c, 0.0) for c in chain[-1:]], kind="r", role=role, name="upd%d" % t)
+        chain.append(i)
+        return i
+
+    w2 = [T["w2_%d" % t] for t in range(NT)]
+    inc = [T["inc%d" % t] for t in range(NT + 1)]
+
+    H = C // 2
+    a0 = dma("s", w2[0][:, 0:F], T.shp[:], 2.3, (), ["s0_%d" % j for j in range(NB)])
+    a1 = dma("s", T.ofi[:], T.ofs[:], 2.0, (), ["ofi"], after=[(a0, -2.3)])
+    a2 = dma("s", T.picw[:, HEAD:HEAD + P], T.pic[:], 3.8, (), ["pic0"], after=[(a1, -2.0)])
+    b0 = dma("y", T.inco[:], T.inc[:], 2.6, (), ["inco"])
+    b1 = dma("y", T.exo[:, 0:H], T.ex[:, 0:H], 3.4, (), ["exo0"], after=[(b0, -2.6)])
+    b2 = dma("y", T.exo[:, H:C], T.ex[:, H:C], 4.2, (), ["exo1"], after=[(b1, -3.4)])
+    b3 = dma("y", T.thi[0:8, :], T.thr[:], 2.0, (), ["thi"], after=[(b2, -4.2)])
+    b4 = dma("y", T.picw[:, HEAD + P:HEAD + 2 * P], T.pic[:], 3.0, ["exo1", "pic0"], ["pic1"], after=[(b3, -2.0)])
+    b5 = dma("y", T.picw[:, 0:HEAD], T.pic[:, P - HEAD:P], 3.0, (), ["pic2"], after=[(b4, -3.0)])
+    dma("y", T.picw[:, HEAD + 2 * P:PW], T.pic[:, 0:HEAD], 3.0, (), ["pic3"], after=[(b5, -3.0)])
+
+    r0 = (rank - 1) % N
+    send(0, r0, inc[0][:, IH:IW], T.inco[:], "ai0", ["inco"])
+    send(1, r0, w2[0][:, F:F + H], T.exo[:, 0:H], "ae0", ["exo0"])
+    first = send(2, r0, w2[0][:, F + H:F + C], T.exo[:, H:C], "ae0", ["exo1"])
+    r1 = (rank - 2) % N
+    if not handed_on(r1, 1):
+        send(3, r1, inc[1][:, IH:IW], T.inco[:], "ai1", ["inco"])
+        send(4, r1, w2[1][:, F:F + C], T.exo[:], "ae1", ["exo0", "exo1"])
+
+    vec(lambda q: q.memset(T.ones[:], 1.0), 128, (), ["ones"], 0.5)
+    vec(lambda q: q.memset(T.mst[:, 0:4 * MW], 0.0), 4 * MW, (), ["m%d" % i for i in range(4)] + ["mm%d" % i for i in range(4)], 0.5)
+    vec(lambda q: q.memset(T.mst[:, 4 * MW:NM * MW], 0.0), (NM - 4) * MW, (),
+        ["m%d" % i for i in range(4, NM)] + ["mm%d" % i for i in range(4, NM)], 0.5)
+    vec(lambda q: q.memset(T.zer[:], 0.0), 4 * W, (), ["zer"], 0.5)
+
+    def sel(out, n, pattern, base, cm=1, op=ALU.is_equal, in_=None, parts=128):
+        src = T.ones[0:parts, 0:n] if in_ is None else in_
+        return lambda q: q.affine_select(out, src, pattern, op, 0.0, base, cm)
+
+    for i, ms in enumerate(MASTERS):
+        o = i * MW
+        if len(ms) == 2:
+            gps(sel(T.mst[:, o + 3:o + 131:4], 32, [[-16, 8], [-ms[1], 2], [-1, 2]], -ms[0]), 32, ["ones"], ["m%d" % i])
+        else:
+            for side in range(2):
+                gps(sel(T.mst[:, o + 6 + side:o + 134:8], 16, [[-16, 8], [-ms[1], 2]], -ms[0] - ms[2] * side), 16, ["ones"],
+                    ["m%d" % i] if side == 0 else ["mm%d" % i])
+
+    def master(ms, u):
+        o = MASTERS.index(ms) * MW + (3 - u if len(ms) == 2 else 6 - 2 * u)
+        return T.mst[:, o:o + 128]
+
+    def mkeys(t, names):
+        ks = [MASTERS.index(SETS[t][nm]) for nm in names]
+        return ["m%d" % k for k in ks] + ["mm%d" % k for k in ks]
+
+    def ident(k):
+        return T.idn[:, 128 * k:128 * k + 128]
+
+    gps(sel(ident(0), 128, [[-1, 128]], 0), 128, ["ones"], ["id0"])
+    scales = [2.0 ** m for m in range(10)] + [2048.0, -2048.0, -2688.0]
+    for k in range(1, 13):
+        act(ident(k), ident(0), ACT.Copy, 128, ["id0"], ["id%d" % k], scale=scales[k])
+    gps(sel(T.bo1[:], 8, [[-16, 8]], 0, op=ALU.is_ge), 8, ["ones"], ["bo1"])
+    gps(sel(T.bo[:], 8, [[16, 8]], 15, cm=-1, op=ALU.is_ge, in_=T.bo1[:]), 8, ["bo1"], ["bo"])
+    gps(sel(T.bot[0:8, :], 128, [[1, 8], [0, 16]], 0, cm=-1, parts=8), 128, ["ones"], ["bot"])
+    for s in range(2):
+        gps(sel(T.hot[:, 4 * B * s:4 * B * (s + 1)], 4 * B, [[-8, 4], [-32, WL], [-2, 4]], -s), 4 * B, ["ones"], ["hot%d" % s])
+    gps(sel(T.hot[:, 8 * B:10 * B], 2 * B, [[-4, 2], [-8, WL], [-1, 4]], -32 * WL), 2 * B, ["ones"], ["hot2"])
+    for t in range(NT + 1):
+        ex_ = SETS[t]["m"] if t < NT else [0] * 10
+        mm([(T.pz[:, t * B:(t + 1) * B], ident(ex_[j]), T.hot[:, j * B:(j + 1) * B], j == 0, j == 9, B) for j in range(10)],
+           ["hot0", "hot1", "hot2"] + ["id%d" % m for m in ex_], ["pz"])
+    act(T.wgt[:], T.pz[:, 0:5 * B], ACT.Copy, 5 * B, (), ["pz", "wgt"])
+    for k, (va, vc) in enumerate(((-8.5, -1.0), (-11.5, -7.0), (3.5, -9.0))):
+        vec(lambda q, k=k, va=va: q.memset(T.tbi[:, k:k + 1], va), 1, (), ["tbi%d" % k])
+        vec(lambda q, k=k, vc=vc: q.memset(T.tbi[32 * WL:128, k:k + 1], vc), 1, (), ["tbi%d" % k])
+    vec(lambda q: q.memset(T.tiny[:], -2.0 ** -100), 4, (), ["tiny"])
+    vec(lambda q: q.tensor_copy(T.thb[0:8, :], T.thi[0:8, :]), 4, ["thi"], ["thb"])
+    mm([(T.pc[:, 0:4], T.bot[0:8, :], T.thb[0:8, :], True, True, 4)], ["bot", "thb"], ["pc"])
+    vec(ts(T.bth[:], T.pc[:, 0:4], -2.0, 21.0, ALU.mult, ALU.add), 4, (), ["pc", "bth"])
+    vec(lambda q: q.tensor_copy(T.off[:], T.ofi[:]), 4, ["ofi"], ["off"])
+    for t in range(1, NT):
+        vec(ts(T.ob[:, (t - 1) * W:t * W], T.zer[:, 0:W], T.off[:, t:t + 1], None, ALU.add), W, ["zer", "off"], ["ob%d" % t], 0.5)
+    gps(lambda q: q.iota(T.pi[:, 0:1], [[0, 1]], 0, 1), 1, (), ["pi"])
+    vec(ts(T.pa[:, 0:1], T.pi[:, 0:1], 15, None, ALU.bitwise_and), 1, ["pi"], ["pa"])
+    vec(ts(T.af[:, 0:1], T.pa[:, 0:1], 2.0, float(RAW), ALU.mult, ALU.add), 1, ["pa"], ["af"])
+    gps(lambda q: q.iota(T.l2[:], [[32, F // 16]], 0, 0, allow_small_or_imprecise_dtypes=True), F // 16, (), ["l2"])
+    gps(lambda q: q.iota(T.kr[:], [[2, SEG]], RAW - 32, 0, allow_small_or_imprecise_dtypes=True), SEG, (), ["kr"])
+    for h in range(4):
+        gps(lambda q, h=h: q.iota(T.io2[:, h * IW // 4:(h + 1) * IW // 4], [[2, IW // 4]], RAW + h * IW // 2, 0,
+                                  allow_small_or_imprecise_dtypes=True), IW // 4, (), ["io2_%d" % h])
+    gps(fill(T.low[:], NB * 2 * B, 2 * KH + RAW), NB * 2 * B, (), ["low%d" % j for j in range(NB)])
+    for j in range(NB):
+        act(T.low[:, (2 * j + 1) * B:(2 * j + 2) * B], T.l2[:, j * B:(j + 1) * B], ACT.Identity, B, ["l2", "af"], ["low%d" % j], bias=T.af[:, 0:1])
+    vec(ts(T.lo3[:, 0:3], T.low[:, B:B + 3], 1.0 / 4096, None, ALU.mult), 3, ["low0"], ["lo3"])
+    for b in range(3):
+        vec(ts(T.cst[:, b * SEG:(b + 1) * SEG - 1], T.kr[:, 0:SEG - 1], T.low[:, B + b:B + b + 1], T.lo3[:, b:b + 1], ALU.is_le, ALU.max), SEG,
+            ["kr", "low0", "lo3"], ["cst%d" % b])
+    gps(fill(T.cst[:, SEG - 1:3 * SEG:SEG], 3, 0), 3, (), ["cst3"])
+    gps(fill(T.eq[:], 3 * SEG, 2), 3 * SEG, (), ["eq%d" % k for k in range(8)])
+    for t in range(NT + 1):
+        gps(fill(inc[t][:, 0:IH], IH, 0), IH, (), ["inc%d" % t])
+    vec(lambda q: q.memset(T.slo[:], 0), NT * 2 * KH, (), ["slo%d" % t for t in range(NT)], 0.5)
+
+    def to_half(j, src, key):
+        for wl in range(WL):
+            vec(ts(T["xh%d" % j][:, wl:FB:WL], src[:, j * FB + 64 * wl:j * FB + 64 * wl + 64], -1024.0, None, ALU.add), 64, [key],
+                ["xh%d_%d" % (j, wl)])
+
+    for j in range(NB):
+        sl = slice(j * FB, (j + 1) * FB)
+        vec(ts(T.ta[:, sl], w2[0][:, sl], T.off[:, 0:1], None, ALU.add), FB, ["s0_%d" % j, "off"], ["ta%d" % j])
+        vec(ts(T.tb[:, sl], T.ta[:, sl], P - 1, None, ALU.bitwise_and), FB, ["ta%d" % j], ["tb%d" % j])
+        to_half(j, T.tb, "tb%d" % j)
+
+    upd = [None] * NT
+    fwd = [None] * (NT + 1)
+
+    def front(t, j):
+        S = SETS[t]
+        k2 = (t * NB + j) % 2
+        pv, kv = T["pv%d" % k2], "pv%d" % k2
+        xh, lst, gb, gx, cmp_, pln = (T["%s%d" % (nm, j)] for nm in ("xh", "lst", "gb", "gx", "cmp", "pln"))
+        xk = ["xh%d_%d" % (j, wl) for wl in range(WL)]
+        if t == 0:
+            win, add_, pk = T.picw[:, HEAD:HEAD + P], 1024.0, ["pic0"]
+        else:
+            win, add_, pk = T.picw[:, 0:PW], 1024.0 + HEAD, ["pic0", "pic1", "pic2", "pic3"]
+        o = 0
+        for h, names in enumerate(SPLIT):
+            pl, kl, n = T["pl%d_%d" % (k2, h)], "pl%d_%d" % (k2, h), len(names)
+            if t == 0:
+                mm([(pl[:, s * W:(s + 1) * W], master(S[nm], u), xh[:, u * W:(u + 1) * W], u == 0, u == 3, W)
+                    for s, nm in enumerate(names) for u in range(4)], mkeys(t, names) + xk, [kl])
+            else:
+                mm([(pl[:, 0:n * W], T.zer[:, 0:128], T.zer[:, 0:n * W], True, False, n * W)] +
+                   [(pl[:, s * W:(s + 1) * W], master(S[nm], u), T.ob[:, (t - 1) * W:t * W], False, False, W)
+                    for s, nm in enumerate(names) for u in range(4)], mkeys(t, names) + ["zer", "ob%d" % t], [kl])
+                mm([(pl[:, s * W:(s + 1) * W], master(S[nm], u), xh[:, u * W:(u + 1) * W], False, s == n - 1 and u == 3, W)
+                    for s, nm in enumerate(names) for u in range(4)], mkeys(t, names) + xk, [kl])
+            vec(ts(lst[:, o * W:(o + n) * W], pl[:, 0:n * W], add_, None, ALU.add), n * W, (), [kl] + ["l%s%d" % (nm, j) for nm in names],
+                name="list%d%d" % (t, j))
+            o += n
+        at = {nm: k * W for k, nm in enumerate([x for names in SPLIT for x in names])}
+        WH, AH = W // HV, 16 // HV
+        for h in range(HV):
+            act(gb[:, 16 * WH * h:16 * WH * (h + 1)], win.indirect(lst[:, at["B"] + WH * h:at["B"] + WH * (h + 1)]), ACT.Copy, 16 * WH,
+                pk + ["lB%d" % j], ["gb%d_%d" % (j, h)], GAT, name="gB%d%d" % (t, j))
+        act(gx[:], win.indirect(lst[:, at["C"]:at["C"] + W]), ACT.Copy, 16 * W, pk + ["lC%d" % j], ["gx%d" % j], GAT, name="gC%d%d" % (t, j))
+        for h in range(HV):
+            for s, op, nm in ((0, ALU.is_gt, "A1"), (1, ALU.is_lt, "A2")):
+                vec(lambda q, s=s, op=op, h=h, nm=nm: q.tensor_tensor(cmp_[:, 32 * WH * h + s:32 * WH * (h + 1):2],
+                                                                      win.indirect(lst[:, at[nm] + WH * h:at[nm] + WH * (h + 1)]),
+                                                                      gb[:, 16 * WH * h:16 * WH * (h + 1)], op),
+                    16 * WH, pk + ["l%s%d" % (nm, j), "gb%d_%d" % (j, h)], ["ca%d_%d_%d" % (j, s, h)], GAT, name="A%d_%d%d" % (s, t, j))
+        mm([(pv[:, 128:128 + 8 * W], ident(10 + side), gx[:, side:16 * W:2], side == 0, side == 1, 8 * W) for side in range(2)],
+           ["id10", "id11", "gx%d" % j], [kv])
+        act(T["cmc%d" % j][:], pv[:, 128:128 + 8 * W], ACT.Sign, 8 * W, ["tiny"], [kv, "cc%d" % j], bias=T.tiny[:, 0:1],
+            name="sC%d%d" % (t, j))
+        mm([(pv[32 * WL:MV, a:128:16], T["cmc%d" % j][:, 8 * WL * a:8 * WL * (a + 1)], T.bo[:], True, True, -8 * WL) for a in range(16)],
+           ["bo", "cc%d" % j], [kv], name="vC%d%d" % (t, j))
+        for h in range(HV):
+            mm([(pv[0:32 * WL, a:128:16], cmp_[:, 32 * WL * a:32 * WL * (a + 1)], T.bo[:], True, True, 8) for a in range(AH * h, AH * (h + 1))],
+               ["bo", "ca%d_0_%d" % (j, h), "ca%d_1_%d" % (j, h)], [kv], name="votes%d%d" % (t, j))
+        for k in (1, 2, 0):
+            act(pln[0:MV, 128 * k:128 * k + 128], pv[0:MV, 0:128], ACT.Sign, 128, ["tbi%d" % k, kv], ["pln%d_%d" % (j, k)],
+                bias=T.tbi[0:MV, k:k + 1], scale=-1.0 if k == 2 else 1.0)
+        mm([(T.pc[:, 0:B], pln[0:MV, 128 * k:128 * k + 128], T.wgt[0:MV, 4 * B:5 * B], k == 1, k == 2, B) for k in (1, 2)],
+           ["wgt", "pln%d_1" % j, "pln%d_2" % j], ["pc"])
+        sg, yr, idx = T["sg%d" % j], T["yr%d" % j], T["idx%d" % j]
+        act(sg[:], T.pc[:, 0:B], ACT.Sign, B, ["bth"], ["pc", "sg%d" % j], bias=T.bth[:, t:t + 1], name="sg%d%d" % (t, j))
+        mm([x for h in range(2) for x in ((T.pz[:, h * B:(h + 1) * B], pln[0:MV, 0:128], T.wgt[0:MV, t * B:(t + 1) * B], True, False, B),
+                                          (T.pz[:, h * B:(h + 1) * B], ident(10 + 2 * h), sg[:], False, True, B))],
+           ["wgt", "pln%d_0" % j, "sg%d" % j, "id10", "id12"], ["pz"])
+        vec(lambda q: q.tensor_tensor(yr[:], T.pz[:, 0:2 * B], T.low[:, 2 * j * B:(2 * j + 2) * B], ALU.max), 2 * B, ["low%d" % j],
+            ["pz", "yr%d" % j])
+        vec(ts(idx[:], yr[:], 0.5, -RAW / 2.0, ALU.mult, ALU.add), 2 * B, ["yr%d" % j], ["idx%d" % j], name="idx%d%d" % (t, j))
+
+    def back(t, j):
+        idx, ga = T["idx%d" % j], T["ga%d" % j]
+        sl = slice(j * FB, (j + 1) * FB)
+        aft = [(first, T_BANK0)] if t == 0 else []
+        act(ga[:], inc[t][:, 0:IW].indirect(idx[:, 0:B]), ACT.Copy, FB, ["idx%d" % j, "inc%d" % t], ["ga%d" % j], GAT,
+            ext=[arr_inc(0)] if t == 0 else [], after=aft, name="g1_%d%d" % (t, j))
+        out, ko = (w2[t + 1][:, sl], "s%d_%d" % (t + 1, j)) if t < NT - 1 else (T.ta[:, sl], "ta%d" % j)
+        vec(lambda q: q.tensor_tensor(out, w2[t][:, 0:F + C].indirect(idx[:, B:2 * B]), ga[:], ALU.add), FB,
+            ["idx%d" % j, "ga%d" % j] + ["s%d_%d" % (t, k) for k in range(NB)], [ko], GAT, ext=[arr_ex(t)], after=aft, name="new%d%d" % (t, j))
+        if t < NT - 1:
+            to_half(j, w2[t + 1], ko)
+        else:
+            vec(ts(T.tb[:, sl], out, P - 1, None, ALU.bitwise_and), FB, [ko], ["tb%d" % j])
+            vec(lambda q: q.tensor_copy(T.ysf[:, sl], T.tb[:, sl]), FB, ["tb%d" % j], ["ysf%d" % j])
+            dma("y", T.ys[:, sl], T.ysf[:, sl], 2.5, ["ysf%d" % j], ())
+
+    def halve(t):
+        pieces, c = [], 3 * t
+        while c < 3 * t + 3:
+            j = c // B
+            e = min(3 * t + 3, (j + 1) * B)
+            pieces.append((j, c - j * B, e - c, c - 3 * t))
+            c = e
+        ik = ["io2_%d" % h for h in range(4)]
+        for pn, (j, c0, nc, pos) in enumerate(pieces):
+            odd = c0 % 2
+            act(T.eq[:, SEG * pos + SEG - 1:SEG * (pos + nc):SEG], T["yr%d" % j][:, c0:c0 + nc], ACT.Copy, nc, ["yr%d" % j], ["eq%d" % (6 + pn)],
+                scale=1.0 / 4096)
+            vec(ts(T["hvo%d" % t][:, 16 * pos:16 * (pos + nc)], T["ga%d" % j][:, 16 * c0:16 * (c0 + nc)], 0.5, -0.25, ALU.mult, ALU.add),
+                16 * nc, ["ga%d" % j], ["hvo%d" % t])
+            for b in range(3):
+                jb, cb = (3 * t + b) // B, (3 * t + b) % B
+                a = SEG * b + 16 + 16 * (pos - odd)
+                act(T.eq[:, a:a + 16 * (nc + odd)], T.io2[:, 0:IW].indirect(T["idx%d" % j][:, c0 - odd:c0 + nc]), ACT.Abs, 16 * (nc + odd),
+                    ik + ["idx%d" % j, "yr%d" % jb], ["eq%d" % (2 * b + pn)], GAT, bias=T["yr%d" % jb][:, cb:cb + 1], scale=-1.0)
+        vec(lambda q: q.tensor_tensor_scan(T.sc[:], T.eq[:], T.cst[:], 1.0, ALU.min, ALU.max), 3 * SEG,
+            ["eq%d" % k for k in range(8)] + ["cst0", "cst1", "cst2", "cst3"], ["sc"])
+        vec(ts(slo(t, 3), T.sc[:, SEG - 1:3 * SEG:SEG], 2048.0, -RAW / 2.0, ALU.mult, ALU.add), 3, ["sc"], ["slo%d" % t])
+
+    def apply_update(t):
+        aft = [(upd[t], T_UPD)] + ([(fwd[t + 1], T_FWD)] if fwd[t + 1] is not None else [])
+        vec(lambda q: q.tensor_copy(inc[t + 1][:, 0:IW].indirect(T["sli%d" % t][:, 0:3]), T["hvi%d" % t][:]), KH, (), ["inc%d" % (t + 1)], SCA,
+            ext=[arr_upd(t), arr_inc(t + 1)], after=aft, name="apply%d" % t)
+
+    jh = [(3 * t + 2) // B for t in range(NT)]
+    for t in range(NT):
+        dst = (rank - 1) % N if t < NT - 1 else (rank + NT) % N
+        if t >= 1:
+            fwd[t + 1] = send(10 + t, dst, inc[t + 1][:, IH:IW], inc[t][:, IH:IW], "ai%d" % (t + 1), ["inc%d" % t])
+        for j in range(NB):
+            front(t, j)
+        for j in range(NB):
+            back(t, j)
+            if j == jh[t]:
+                halve(t)
+                if t == 0 and handed_on(r0, 1):
+                    send(5, r0, inc[1][:, IH:IW], inc[0][:, IH:IW], "ai1", ["inc0"], ext=[arr_inc(0)], after=[(first, T_BANK0)])
+                    send(6, r0, w2[1][:, F:F + C], w2[0][:, F:F + C], "ae1", (), ext=[arr_ex(0)])
+                upd[t] = send_update(20 + t, dst, t)
+                if t == 0:
+                    late = [tt for tt in (2, 3) if not handed_on((rank - 1 - tt) % N, tt)]
+                    for k, tt in enumerate(late):
+                        send(7 + k, (rank - 1 - tt) % N, w2[tt][:, F:F + C], T.exo[:], "ae%d" % tt, ["exo0", "exo1"])
+                if t in (0, 1) and handed_on(r0, t + 2):
+                    send(30 + t, r0, w2[t + 2][:, F:F + C], w2[t + 1][:, F:F + C], "ae%d" % (t + 2), (), ext=[arr_ex(t + 1)])
+        apply_update(t)
+    dma("y", T.yi[:], inc[NT][:, IH:IW], 2.8, ["inc%d" % NT], ())
+
+    order = call_order(nodes)
+    INFO[rank] = (nodes, order)
+    counts, waited = {}, {}
+    for i in order:
+        nd = nodes[i]
+        q, e = Q[nd["eng"]], nd["eng"]
+        need = {}
+        for p in nd["dep"]:
+            need[nodes[p]["sem"]] = max(need.get(nodes[p]["sem"], 0), nodes[p]["val"])
+        for s, v in nd["ext"]:
+            need[s] = max(need.get(s, 0), v)
+            totals[s] = max(totals.get(s, 0), v)
+        for s in sorted(need):
+            if waited.get((e, s), 0) < need[s]:
+                q.wait_ge(T.sem[s], int(need[s]))
+                waited[(e, s)] = need[s]
+        ins = nd["fn"](q)
+        if nd["kind"] == "d":
+            ins[0].then_inc(T.sem[nd["sem"]], 16)
+            nd["val"] = totals[nd["sem"]] = 16
+        elif nd["kind"] == "c":
+            nd["sem"] = QSEM[e]
+            for x in ins:
+                x.then_inc(T.sem[nd["sem"]], 1)
+            nd["val"] = counts[nd["sem"]] = counts.get(nd["sem"], 0) + len(ins)
+    totals.update(counts)
+    for s in sorted(totals):
+        if max([v for (e, k), v in waited.items() if k == s] + [0]) < totals[s]:
+            g.wait_ge(T.sem[s], int(totals[s]))

@@ -5,20 +5,28 @@ ALU = AluOpType
 ACT = ActivationFunctionType
 
 P, F, C, NT, KH, D0 = 2048, 384, 1024, 4, 48, 6
-WL = 3
-FB = 64 * WL
-NB = F // FB
-W = 16 * WL
-B = 4 * WL
-MV = 40 * WL
-HV = 2
-SPLIT = (("B",), ("A1", "C", "A2"))
-HEAD = 768
+MODE = "six"
+PICV = "yyyy"
+GO = 1
+XP = 99
+LOADS = "isep"
+WIDE0 = 1
+NB = 2
+FB = F // NB
+W = FB // 4
+B = FB // 16
+WL = FB // 64
+MA = 8 * B
+MV = 10 * B
+NAMES = ("B", "A1", "A2", "C")
+STEP = 256
+HEAD = STEP * (NT - 1)
 PW = 2 * P + 2 * HEAD
-IH = 64
-IW = IH + C
-MW = 136
-RAW = 897
+SP = C + 16
+IW = SP + KH
+MW = 144
+RAW = C - 1
+BIG = 2048.0
 SEG = 65
 
 SETS = []
@@ -30,7 +38,7 @@ for _t in range(NT):
     SETS.append({"B": (_d, _x), "A1": (0, _x), "A2": (2 * _d, _x), "C": (_rest[0], _rest[1] - _rest[0], _d), "m": _m + _rest})
 MASTERS = []
 for _t in range(NT):
-    for _n in ("B", "C", "A1", "A2"):
+    for _n in NAMES:
         if SETS[_t][_n] not in MASTERS:
             MASTERS.append(SETS[_t][_n])
 NM = len(MASTERS)
@@ -42,40 +50,39 @@ SCRATCH = {
     "ofi": ("sbuf", [128, 4], "int32"),
     "off": ("sbuf", [128, 4], "float32"),
     "thi": ("sbuf", [128, 4], "int32"),
-    "thb": ("sbuf", [128, 4], "bfloat16"),
-    "bth": ("sbuf", [128, 4], "float32"),
+    "thx": ("sbuf", [128, 128 - MA], "bfloat16"),
     "ob": ("sbuf", [128, 3 * W], "float16"),
+    "obl": ("sbuf", [128, 12 * W], "float16"),
     "ta": ("sbuf", [128, F], "int32"),
     "tb": ("sbuf", [128, F], "int32"),
     "ysf": ("sbuf", [128, F], "float32"),
     "mst": ("sbuf", [128, NM * MW], "bfloat16"),
     "ones": ("sbuf", [128, 128], "bfloat16"),
-    "zer": ("sbuf", [128, 4 * W], "bfloat16"),
-    "idn": ("sbuf", [128, 13 * 128], "bfloat16"),
-    "bo": ("sbuf", [128, 8], "bfloat16"),
-    "bo1": ("sbuf", [128, 8], "bfloat16"),
+    "zer": ("sbuf", [128, 128], "bfloat16"),
+    "idn": ("sbuf", [128, 12 * 128], "bfloat16"),
+    "bos": ("sbuf", [128, 48], "bfloat16"),
     "bot": ("sbuf", [128, 128], "bfloat16"),
-    "hot": ("sbuf", [128, 10 * B], "bfloat16"),
-    "wgt": ("sbuf", [128, 5 * B], "bfloat16"),
-    "tbi": ("sbuf", [128, 4], "float32"),
-    "tiny": ("sbuf", [128, 4], "float32"),
+    "hot": ("sbuf", [128, 24 * B], "bfloat16"),
+    "wgt": ("sbuf", [128, 36 * B], "bfloat16"),
+    "gs": ("sbuf", [128, 256], "bfloat16"),
+    "col": ("sbuf", [128, 8], "float32"),
     "pi": ("sbuf", [128, 4], "int32"),
     "pa": ("sbuf", [128, 4], "int32"),
     "af": ("sbuf", [128, 4], "float32"),
     "l2": ("sbuf", [128, F // 16], "float32"),
-    "low": ("sbuf", [128, NB * 2 * B], "float32"),
-    "lo3": ("sbuf", [128, 4], "float32"),
+    "low": ("sbuf", [128, NB * 6 * B], "float32"),
+    "own": ("sbuf", [128, 4], "float32"),
     "kr": ("sbuf", [128, SEG], "float32"),
     "cst": ("sbuf", [128, 3 * SEG], "float32"),
     "eq": ("sbuf", [128, 3 * SEG], "float32"),
     "sc": ("sbuf", [128, 3 * SEG], "float32"),
     "io2": ("sbuf", [128, IW], "float32"),
-    "slo": ("sbuf", [128, NT * 2 * KH], "uint16"),
-    "pc": ("psum", [128, 512], "float32"),
-    "pz": ("psum", [128, 512], "float32"),
 }
+for _n in ("pl0", "pl1", "pv0", "pv1", "pd", "pw", "pz0", "pz1"):
+    SCRATCH[_n] = ("psum", [128, 512], "float32")
 for _t in range(NT):
-    SCRATCH["w2_%d" % _t] = ("sbuf", [128, F + C], "int32")
+    SCRATCH["w2_%d" % _t] = ("sbuf", [128, C + F], "int32")
+    SCRATCH["slo%d" % _t] = ("sbuf", [128, 2 * KH], "uint16")
     SCRATCH["sli%d" % _t] = ("sbuf", [128, 2 * KH], "uint16")
     SCRATCH["hvo%d" % _t] = ("sbuf", [128, KH], "int32")
     SCRATCH["hvi%d" % _t] = ("sbuf", [128, KH], "int32")
@@ -89,75 +96,24 @@ for _j in range(NB):
     SCRATCH["cmp%d" % _j] = ("sbuf", [128, 32 * W], "bfloat16")
     SCRATCH["cmc%d" % _j] = ("sbuf", [128, 8 * W], "bfloat16")
     SCRATCH["pln%d" % _j] = ("sbuf", [128, 3 * 128], "bfloat16")
-    SCRATCH["sg%d" % _j] = ("sbuf", [128, B], "bfloat16")
-    SCRATCH["yr%d" % _j] = ("sbuf", [128, 2 * B], "float32")
+    SCRATCH["yr%d" % _j] = ("sbuf", [128, 6 * B], "float32")
     SCRATCH["idx%d" % _j] = ("sbuf", [128, 2 * B], "uint16")
     SCRATCH["ga%d" % _j] = ("sbuf", [128, FB], "float32")
-for _j in range(2):
-    SCRATCH["pl%d_0" % _j] = ("psum", [128, 512], "float32")
-    SCRATCH["pl%d_1" % _j] = ("psum", [128, 512], "float32")
-    SCRATCH["pv%d" % _j] = ("psum", [128, 512], "float32")
 
-SEMAPHORES = (["qv", "qs", "qp", "qg", "sent"] + ["d%d" % i for i in range(16)] + ["ae%d" % t for t in range(NT)]
+SEMAPHORES = (["qv", "qs", "qp", "qg", "sent", "go"] + ["d%d" % i for i in range(20)] + ["ae%d" % t for t in range(NT)]
               + ["ai%d" % t for t in range(NT + 1)] + ["au%d" % t for t in range(NT)])
 
-CYC, FIX, GAT, SCA, PEC, HOP = 0.00104, 0.07, 1.56, 3.8, 0.0006, 0.08
-T_BANK0, T_UPD, T_FWD = 7.5, 4.0, 6.0
-LOOK = 0.05
-ORDER = [3, 71, 0, 4, 10, 1, 2, 5, 6, 7, 8, 9, 32, 61, 11, 12, 13, 62, 94, 57, 67, 95, 96, 70, 97, 99, 98, 15, 45, 14, 48, 50, 21, 89, 49,
-         17, 16, 1000, 43, 39, 34, 37, 33, 40, 35, 41, 36, 38, 44, 42, 72, 100, 18, 1001, 1002, 77, 30, 24, 47, 1003, 20, 87, 80, 46, 76,
-         74, 1004, 22, 26, 28, 19, 79, 25, 88, 78, 75, 51, 105, 106, 63, 101, 59, 58, 68, 109, 102, 110, 52, 107, 64, 60, 103, 108, 104,
-         113, 53, 129, 131, 130, 112, 65, 73, 114, 66, 111, 116, 133, 117, 54, 132, 115, 137, 136, 134, 135, 139, 138, 118, 119, 55, 120,
-         140, 122, 56, 82, 121, 124, 171, 141, 123, 125, 142, 126, 143, 144, 174, 81, 83, 127, 128, 153, 154, 156, 157, 155, 147, 145,
-         146, 148, 172, 84, 86, 85, 173, 162, 160, 161, 158, 175, 159, 163, 164, 176, 177, 180, 149, 200, 197, 150, 69, 181, 151, 152,
-         1005, 1006, 1020, 23, 90, 92, 1007, 91, 179, 178, 183, 182, 184, 185, 165, 241, 186, 187, 188, 166, 168, 167, 169, 198, 199,
-         190, 189, 191, 192, 193, 194, 170, 195, 196, 201, 203, 228, 223, 202, 230, 232, 204, 205, 231, 224, 227, 225, 226, 244, 242,
-         245, 207, 243, 229, 208, 246, 247, 233, 206, 234, 209, 250, 251, 210, 270, 211, 212, 267, 213, 249, 254, 214, 248, 255, 256,
-         31, 27, 1030, 29, 1011, 1021, 1031, 93, 216, 215, 217, 253, 252, 218, 257, 219, 220, 221, 222, 235, 236, 237, 239, 238, 240,
-         258, 311, 259, 260, 261, 262, 263, 264, 265, 298, 266, 293, 268, 269, 271, 294, 272, 295, 296, 297, 273, 276, 274, 278, 314,
-         337, 312, 315, 313, 277, 316, 275, 301, 318, 280, 317, 281, 340, 279, 323, 282, 283, 284, 319, 302, 300, 321, 299, 320, 303,
-         304, 286, 285, 324, 287, 288, 289, 290, 325, 322, 326, 327, 328, 1012, 1022, 291, 292, 305, 306, 309, 308, 307, 338, 339, 329,
-         330, 331, 343, 332, 341, 333, 344, 334, 342, 347, 335, 336, 310, 346, 348, 345, 368, 370, 372, 371, 363, 373, 374, 369, 349,
-         364, 365, 366, 350, 351, 352, 353, 354, 356, 355, 358, 357, 359, 360, 361, 362, 375, 376, 377, 1013, 1023, 380, 367, 381, 378,
-         379]
-INFO = {}
+CUTS = (0, 16, 32, 48)
+BCUTS = (0, 16, 32, 48)
+CCUTS = (0, 16, 48)
+START = "loads first m0 fills z1 off heads z2 z3 prep b0 b1 b2 go counts hot"
+SLOT = "a1 hvo-- gB1 slo-- a0 OB+ vC0- pln0- a2 Z- gB2 half-- OR+ yr- job apply- gC0 idx- a4 ga- store-- new- a5 gC1 LB+ eq- listB+ LR+ D gB0+ a3 listR+ scan- sC vA0 jobc"
+OTHER = {-1: "LB+ LR+ listB+ ob thr gB0+ listR+ LB++ gB1+ listB++ gB2+ LR++ floors cst copies wc w0", 0: "gC1 a0 a3 gC0 bos m1 bank1 io2 m2 hand1 m3 listR+ a1 a2 gB0+ w0c D rows gB1+ a5 sC a4 wd vA0", 1: "a3 vC0- a0 gC0 a1 o1 pln0- Z- o1c gB2 yr- idx- job a2 OB+ ga- OR+ new- LB+ eq- listB+ gC1 a5 LR+ gB0+ listR+ jobc D a4 sC scan- vA0", 7: "a1 apply- a0 vC0- gB2 gB1 a5 pln0- gC0 Z- a2 yr- gC1 D a3 half-- idx- eq- a4 sC scan- ga- vA0 hvo- slo- new-", 8: "vC0- pln0- half-- Z- yr- idx- store-- ga- new-", 9: "half-- store--"}
+JOBS = {1: "w1", 2: "o2", 3: "w2", 4: "o3", 5: "w3"}
 
 
-def list_order(nodes):
-    n = len(nodes)
-    succ = [[] for _ in range(n)]
-    left = [0] * n
-    for i, nd in enumerate(nodes):
-        for p, lat in nd["pre"]:
-            succ[p].append((i, lat))
-            left[i] += 1
-    prio = [0.0] * n
-    for i in range(n - 1, -1, -1):
-        prio[i] = nodes[i]["cost"] + nodes[i]["lat"] + max([prio[s] + lat for s, lat in succ[i]] + [0.0])
-    ready = [0.0] * n
-    free, order, cand = {}, [], [i for i in range(n) if left[i] == 0]
-    while cand:
-        first = min(cand, key=lambda i: (max(ready[i], free.get(nodes[i]["eng"], 0.0)), -prio[i], i))
-        e = nodes[first]["eng"]
-        t = max(ready[first], free.get(e, 0.0))
-        pick = max([i for i in cand if nodes[i]["eng"] == e and ready[i] <= t + LOOK], key=lambda i: (prio[i], -i))
-        t = max(t, ready[pick])
-        cand.remove(pick)
-        free[e] = t + nodes[pick]["cost"]
-        order.append(pick)
-        for s, lat in succ[pick]:
-            ready[s] = max(ready[s], free[e] + nodes[pick]["lat"] + lat)
-            left[s] -= 1
-            if left[s] == 0:
-                cand.append(s)
-    return order
-
-
-def call_order(nodes):
-    pos = {k: i for i, k in enumerate(ORDER)}
-    if all(nd["key"] in pos for nd in nodes) and all(pos[nodes[p]["key"]] < pos[nd["key"]] for nd in nodes for p, _ in nd["pre"]):
-        return sorted(range(len(nodes)), key=lambda i: pos[nodes[i]["key"]])
-    return list_order(nodes)
+def bits(es):
+    return sum(1 << e for e in es)
 
 
 def rank_program(g, core, T, topo):
@@ -167,64 +123,77 @@ def rank_program(g, core, T, topo):
     cores = list(T.cores)
     N = len(cores)
     Q = {"g": g, "v": g.vector, "s": g.scalar, "p": g.tensor, "y": g.sync}
-    QSEM = {"g": "qg", "v": "qv", "s": "qs", "p": "qp"}
-    nodes, last_w, readers = [], {}, {}
-    ndma, nkey = [0], [0]
-    totals = {}
+    last_w, readers, totals, waited = {}, {}, {}, {}
+    ndma = [0]
 
-    def add(eng, fn, cost, reads=(), writes=(), ext=(), after=(), lat=0.0, kind="c", name="", cm=None, role=None):
-        i = len(nodes)
-        dep = set()
+    def add(eng, fn, reads=(), writes=(), ext=(), kind="c"):
+        need = {}
+        for k in list(reads) + list(writes):
+            for s, v in last_w.get(k, []) + (readers.get(k, []) if k in writes else []):
+                need[s] = max(need.get(s, 0), v)
         for k in reads:
-            if k in last_w:
-                dep.add(last_w[k])
-        for k in writes:
-            if k in last_w:
-                dep.add(last_w[k])
-            dep.update(readers.get(k, []))
-        for k in reads:
-            readers.setdefault(k, []).append(i)
-        for k in writes:
-            last_w[k] = i
-            readers[k] = []
-        dep.discard(i)
-        nd = {"eng": eng, "fn": fn, "cost": cost, "dep": sorted(dep), "ext": list(ext), "lat": lat, "kind": kind,
-              "pre": [(p, HOP) for p in sorted(dep)] + list(after), "name": name, "cm": cm}
+            assert k in last_w, k
+        for s, v in ext:
+            need[s] = max(need.get(s, 0), v)
+            totals[s] = max(totals.get(s, 0), v)
+        q = Q[eng]
+        if eng == "p":
+            need.pop("qp", None)
+        for s in sorted(need):
+            if waited.get((eng, s), 0) < need[s]:
+                q.wait_ge(T.sem[s], int(need[s]))
+                waited[(eng, s)] = need[s]
+        ins = fn(q)
+        if kind == "r":
+            return
         if kind == "d":
-            nd["sem"] = "d%d" % ndma[0]
+            sem, step = "d%d" % ndma[0], 16
             ndma[0] += 1
-        if role is None:
-            nd["key"] = nkey[0]
-            nkey[0] += 1
         else:
-            nd["key"] = 1000 + role
-        nodes.append(nd)
-        return i
+            sem, step = "q" + eng, 1
+        for x in ins:
+            x.then_inc(T.sem[sem], step)
+        totals[sem] = totals.get(sem, 0) + step * len(ins)
+        for k in reads:
+            readers.setdefault(k, []).append((sem, totals[sem]))
+        for k in writes:
+            last_w[k] = [(sem, totals[sem])]
+            readers[k] = []
 
-    def vec(fn, n, reads, writes, c=1.0, **kw):
-        return add("v", lambda q: [fn(q)], FIX + max(n * c, 32) * CYC, reads, writes, cm=(n, c), **kw)
+    def vec(fn, reads, writes, **kw):
+        add("v", lambda q: [fn(q)], reads, writes, **kw)
 
-    def act(out, in_, func, n, reads, writes, c=1.0, bias=0.0, scale=1.0, **kw):
-        return add("s", lambda q: [q.activation(out, in_, func, bias=bias, scale=scale)], FIX + max(n * c, 32) * CYC, reads, writes,
-                   cm=(n, c), **kw)
+    def act(out, in_, func, reads, writes, bias=0.0, scale=1.0, **kw):
+        add("s", lambda q: [q.activation(out, in_, func, bias=bias, scale=scale)], reads, writes, **kw)
 
-    def mm(lst, reads, writes, **kw):
-        cyc = sum(max(64, x[5]) if x[5] > 0 else -x[5] for x in lst)
-        return add("p", lambda q: [q.matmul(o, l, r, a, b) for o, l, r, a, b, _ in lst], cyc * PEC + 0.1, reads, writes, cm=cyc, **kw)
+    def mm(lst, reads, writes):
+        add("p", lambda q: [q.matmul(o, l, r, a, b) for o, l, r, a, b in lst], reads, writes)
 
-    def gps(fn, n, reads, writes, **kw):
-        return add("g", lambda q: [fn(q)], 0.2 + 2 * n * CYC, reads, writes, **kw)
+    def group(lst):
+        return [(o, l, r, k == 0, k == len(lst) - 1) for k, (o, l, r) in enumerate(lst)]
 
-    def dma(eng, out, in_, lat, reads, writes, **kw):
-        return add(eng, lambda q: [q.dma_start(out, in_)], 0.1, reads, writes, lat=lat, kind="d", **kw)
+    def gps(fn, reads, writes):
+        add("g", lambda q: [fn(q)], reads, writes)
+
+    def dma(eng, out, in_, reads, writes, **kw):
+        add(eng, lambda q: [q.dma_start(out, in_)], reads, writes, kind="d", **kw)
 
     def ts(out, in0, s1, s2, op0, op1=None):
         if op1 is None:
             return lambda q: q.tensor_scalar(out, in0, s1, None, op0)
         return lambda q: q.tensor_scalar(out, in0, s1, s2, op0, op1)
 
-    def fill(out, n, value):
-        return lambda q: q.iota(out, [[0, n]], value, 0, allow_small_or_imprecise_dtypes=True)
+    def fill(out, value, keys):
+        vec(lambda q: q.memset(out, value), (), keys)
+
+    def sfill(out, value, keys):
+        act(out, T.idn[:, 0:out.shape[1]], ACT.Identity, ["id%d" % k for k in range(5)], keys, scale=0.0, bias=value)
+
+    def iota(out, pattern, base, keys):
+        gps(lambda q: q.iota(out, pattern, base, 0, allow_small_or_imprecise_dtypes=True), (), keys)
+
+    def sel(out, n, pattern, base, keys, cm=1, parts=128):
+        gps(lambda q: q.affine_select(out, T.ones[0:parts, 0:n], pattern, ALU.is_equal, 0.0, base, cm), ["ones"], keys)
 
     def same_chip(a, b):
         return b in topo.cores_of(a)
@@ -232,13 +201,10 @@ def rank_program(g, core, T, topo):
     def far_mask(a):
         return [topo.mask(a, b) for b in cores if not same_chip(a, b)][0]
 
-    def engines(a, b):
-        if same_chip(a, b):
-            return [e for e in topo.engines(a, b) if not far_mask(a) >> e & 1]
+    def engines(a, b, wide=False):
+        if same_chip(a, b) and wide != 1:
+            return [e for e in topo.engines(a, b) if (far_mask(a) >> e & 1) == (wide == 2)]
         return list(topo.engines(a, b))
-
-    def bits(es):
-        return sum(1 << e for e in es)
 
     def handed_on(r, t):
         return t >= 1 and same_chip(cores[r], cores[(r + 1) % N])
@@ -253,85 +219,95 @@ def rank_program(g, core, T, topo):
         return (r + 1) % N if t < NT - 1 else (r - NT) % N
 
     def arr_ex(t):
-        return ("ae%d" % t, (2 if t == 0 else 1) * len(engines(cores[src_ex(rank, t)], core)))
+        return ("ae%d" % t, (2 if t == 0 else 1) * len(engines(cores[src_ex(rank, t)], core, WIDE0 and t == 0)))
 
     def arr_inc(t):
-        return ("ai%d" % t, len(engines(cores[src_inc(rank, t)], core)))
+        return ("ai%d" % t, len(engines(cores[src_inc(rank, t)], core, WIDE0 and t == 0)))
 
     def arr_upd(t):
         return ("au%d" % t, len(engines(cores[src_upd(rank, t)], core)))
 
-    chain = []
-
-    def send(role, r, out, in_, sem, reads, ext=(), after=()):
-        es = engines(core, cores[r])
-        rid, pid = topo.addr(cores[r], core)
+    def send(dst, out, in_, sem, reads, ext=(), wide=False):
+        es = engines(core, dst, wide)
+        rid, pid = topo.addr(dst, core)
         totals["sent"] = totals.get("sent", 0) + len(es)
-        i = add("g", lambda q: [q.remote_dma(out, in_, T.sem[sem], T.sem.sent, pid, rid, bits(es))], 0.5, reads, (), ext=ext,
-                after=[(c, 0.0) for c in chain[-1:]] + list(after), kind="r", role=role, name="r%d" % role)
-        chain.append(i)
-        return i
+        add("g", lambda q: q.remote_dma(out, in_, T.sem[sem], T.sem.sent, pid, rid, bits(es)), reads, (), ext=ext, kind="r")
 
-    def slo(t, n):
-        return T.slo[:, 2 * KH * t:2 * KH * t + n]
-
-    def send_update(role, r, t):
-        es = engines(core, cores[r])
-        rid, pid = topo.addr(cores[r], core)
-        h = len(es) // 2
-        totals["sent"] = totals.get("sent", 0) + len(es)
-        tr = [RemoteDMATransfer(dst_ids=[DstId(rid=rid, pnc=pid)], dma_engine_mask=bits(e), remote_sem=T.sem["au%d" % t], src=a, dst=b)
-              for e, a, b in ((es[:h], slo(t, 2 * KH), T["sli%d" % t][:]), (es[h:], T["hvo%d" % t][:], T["hvi%d" % t][:]))]
-        i = add("g", lambda q: [q.remote_dma_fused(tr, local_sem=T.sem.sent)], 0.5, ["slo%d" % t, "hvo%d" % t], (),
-                after=[(c, 0.0) for c in chain[-1:]], kind="r", role=role, name="upd%d" % t)
-        chain.append(i)
-        return i
+    def ring(t):
+        return cores[(rank - 1) % N if t < NT - 1 else (rank + NT) % N]
 
     w2 = [T["w2_%d" % t] for t in range(NT)]
     inc = [T["inc%d" % t] for t in range(NT + 1)]
-
     H = C // 2
-    a0 = dma("s", w2[0][:, 0:F], T.shp[:], 2.3, (), ["s0_%d" % j for j in range(NB)])
-    a1 = dma("s", T.ofi[:], T.ofs[:], 2.0, (), ["ofi"], after=[(a0, -2.3)])
-    a2 = dma("s", T.picw[:, HEAD:HEAD + P], T.pic[:], 3.8, (), ["pic0"], after=[(a1, -2.0)])
-    b0 = dma("y", T.inco[:], T.inc[:], 2.6, (), ["inco"])
-    b1 = dma("y", T.exo[:, 0:H], T.ex[:, 0:H], 3.4, (), ["exo0"], after=[(b0, -2.6)])
-    b2 = dma("y", T.exo[:, H:C], T.ex[:, H:C], 4.2, (), ["exo1"], after=[(b1, -3.4)])
-    b3 = dma("y", T.thi[0:8, :], T.thr[:], 2.0, (), ["thi"], after=[(b2, -4.2)])
-    b4 = dma("y", T.picw[:, HEAD + P:HEAD + 2 * P], T.pic[:], 3.0, ["exo1", "pic0"], ["pic1"], after=[(b3, -2.0)])
-    b5 = dma("y", T.picw[:, 0:HEAD], T.pic[:, P - HEAD:P], 3.0, (), ["pic2"], after=[(b4, -3.0)])
-    dma("y", T.picw[:, HEAD + 2 * P:PW], T.pic[:, 0:HEAD], 3.0, (), ["pic3"], after=[(b5, -3.0)])
+    r0, r1 = (rank - 1) % N, (rank - 2) % N
 
-    r0 = (rank - 1) % N
-    send(0, r0, inc[0][:, IH:IW], T.inco[:], "ai0", ["inco"])
-    send(1, r0, w2[0][:, F:F + H], T.exo[:, 0:H], "ae0", ["exo0"])
-    first = send(2, r0, w2[0][:, F + H:F + C], T.exo[:, H:C], "ae0", ["exo1"])
-    r1 = (rank - 2) % N
-    if not handed_on(r1, 1):
-        send(3, r1, inc[1][:, IH:IW], T.inco[:], "ai1", ["inco"])
-        send(4, r1, w2[1][:, F:F + C], T.exo[:], "ae1", ["exo0", "exo1"])
+    def loads():
+        what = {"s": [(w2[0][:, C:C + F], T.shp[:], ["s0_%d" % j for j in range(NB)])], "p": [(T.picw[:, HEAD:HEAD + P], T.pic[:], ["pic0"])],
+                "i": [(T.inco[:], T.inc[:], ["own0"])],
+                "e": [(T.exo[:, 0:H], T.ex[:, 0:H], ["own1"]), (T.exo[:, H:C], T.ex[:, H:C], ["own2"])]}
+        dma("s", T.ofi[:], T.ofs[:], (), ["ofi"])
+        for out, in_, keys in [x for k in LOADS for x in what[k]]:
+            dma("y", out, in_, (), keys)
+        dma("s", T.thi[0:8, :], T.thr[:], (), ["thi"])
 
-    vec(lambda q: q.memset(T.ones[:], 1.0), 128, (), ["ones"], 0.5)
-    vec(lambda q: q.memset(T.mst[:, 0:4 * MW], 0.0), 4 * MW, (), ["m%d" % i for i in range(4)] + ["mm%d" % i for i in range(4)], 0.5)
-    vec(lambda q: q.memset(T.mst[:, 4 * MW:NM * MW], 0.0), (NM - 4) * MW, (),
-        ["m%d" % i for i in range(4, NM)] + ["mm%d" % i for i in range(4, NM)], 0.5)
-    vec(lambda q: q.memset(T.zer[:], 0.0), 4 * W, (), ["zer"], 0.5)
-
-    def sel(out, n, pattern, base, cm=1, op=ALU.is_equal, in_=None, parts=128):
-        src = T.ones[0:parts, 0:n] if in_ is None else in_
-        return lambda q: q.affine_select(out, src, pattern, op, 0.0, base, cm)
-
-    for i, ms in enumerate(MASTERS):
-        o = i * MW
-        if len(ms) == 2:
-            gps(sel(T.mst[:, o + 3:o + 131:4], 32, [[-16, 8], [-ms[1], 2], [-1, 2]], -ms[0]), 32, ["ones"], ["m%d" % i])
+    def bank0(k):
+        if k == 0:
+            send(cores[r0], inc[0][:, 0:C], T.inco[:], "ai0", ["own0"], wide=WIDE0)
         else:
-            for side in range(2):
-                gps(sel(T.mst[:, o + 6 + side:o + 134:8], 16, [[-16, 8], [-ms[1], 2]], -ms[0] - ms[2] * side), 16, ["ones"],
-                    ["m%d" % i] if side == 0 else ["mm%d" % i])
+            send(cores[r0], w2[0][:, (k - 1) * H:k * H], T.exo[:, (k - 1) * H:k * H], "ae0", ["own%d" % k], wide=WIDE0)
+
+    def go():
+        add("g", lambda q: q.sem_inc(T.sem.go, 1), kind="r")
+
+    def copies():
+        dma("y", T.picw[:, HEAD - STEP:HEAD], T.pic[:, P - STEP:P], (), ["pic2"])
+        dma("y", T.picw[:, HEAD + 2 * P:HEAD + 2 * P + STEP], T.pic[:, 0:STEP], (), ["pic3"])
+        dma("y", T.picw[:, HEAD + P:HEAD + 2 * P], T.pic[:], (), ["pic1_%d" % k for k in range(4)], ext=[("go", 1)])
+        dma("y", T.picw[:, 0:HEAD - STEP], T.pic[:, P - HEAD:P - STEP], (), ["pic4"], ext=[("go", 1)])
+        dma("y", T.picw[:, HEAD + 2 * P + STEP:PW], T.pic[:, STEP:HEAD], (), ["pic5"])
+
+    def again(k):
+        a, n = HEAD + k * P // 4, P // 4
+        out, in_, key = T.picw[:, a + P:a + P + n], T.picw[:, a:a + n], ["pic1_%d" % k]
+        if PICV[k] == "y":
+            dma("y", out, T.pic[:, k * n:(k + 1) * n], (), key, ext=[("go", 1)] if GO else [])
+        elif PICV[k] == "v":
+            vec(lambda q: q.tensor_copy(out, in_), ["pic0"], key)
+        else:
+            act(out, in_, ACT.Copy, ["pic0"], key)
+
+    def bank1():
+        if not handed_on(r1, 1):
+            send(cores[r1], inc[1][:, 0:C], T.inco[:], "ai1", ["own0"])
+            send(cores[r1], w2[1][:, 0:C], T.exo[:], "ae1", ["own1", "own2"])
+        if handed_on(r0, 1):
+            send(cores[r0], inc[1][:, 0:C], inc[0][:, 0:C], "ai1", (), ext=[arr_inc(0)])
+
+    def hand_on(t):
+        if handed_on(r0, t):
+            send(cores[r0], w2[t][:, 0:C], w2[t - 1][:, 0:C], "ae%d" % t, (), ext=[arr_ex(t - 1)], wide=0)
+
+    def fresh(t):
+        return [nm for nm in NAMES if all(SETS[t][nm] != SETS[k][nm] for k in range(t))]
+
+    def blank(t):
+        ks = [MASTERS.index(SETS[t][nm]) for nm in fresh(t)]
+        (fill if t < 2 else sfill)(T.mst[:, ks[0] * MW:(ks[-1] + 1) * MW], 0.0, ["m%d" % i for i in ks] + ["mm%d" % i for i in ks])
+
+    def masters(t):
+        for nm in fresh(t):
+            ms = SETS[t][nm]
+            i = MASTERS.index(ms)
+            o = i * MW
+            if len(ms) == 2:
+                sel(T.mst[:, o + 3:o + 131:4], 32, [[-16, 8], [-ms[1], 2], [-1, 2]], -ms[0], ["m%d" % i])
+            else:
+                for side in range(2):
+                    sel(T.mst[:, o + 12 + side:o + 140:2], 64, [[-16, 8], [-1000, 4], [-ms[1], 2]], -ms[0] - ms[2] * side,
+                        ["m%d" % i] if side == 0 else ["mm%d" % i])
 
     def master(ms, u):
-        o = MASTERS.index(ms) * MW + (3 - u if len(ms) == 2 else 6 - 2 * u)
+        o = MASTERS.index(ms) * MW + (3 - u if len(ms) == 2 else 12 - 4 * u)
         return T.mst[:, o:o + 128]
 
     def mkeys(t, names):
@@ -341,220 +317,304 @@ def rank_program(g, core, T, topo):
     def ident(k):
         return T.idn[:, 128 * k:128 * k + 128]
 
-    gps(sel(ident(0), 128, [[-1, 128]], 0), 128, ["ones"], ["id0"])
-    scales = [2.0 ** m for m in range(10)] + [2048.0, -2048.0, -2688.0]
-    for k in range(1, 13):
-        act(ident(k), ident(0), ACT.Copy, 128, ["id0"], ["id%d" % k], scale=scales[k])
-    gps(sel(T.bo1[:], 8, [[-16, 8]], 0, op=ALU.is_ge), 8, ["ones"], ["bo1"])
-    gps(sel(T.bo[:], 8, [[16, 8]], 15, cm=-1, op=ALU.is_ge, in_=T.bo1[:]), 8, ["bo1"], ["bo"])
-    gps(sel(T.bot[0:8, :], 128, [[1, 8], [0, 16]], 0, cm=-1, parts=8), 128, ["ones"], ["bot"])
-    for s in range(2):
-        gps(sel(T.hot[:, 4 * B * s:4 * B * (s + 1)], 4 * B, [[-8, 4], [-32, WL], [-2, 4]], -s), 4 * B, ["ones"], ["hot%d" % s])
-    gps(sel(T.hot[:, 8 * B:10 * B], 2 * B, [[-4, 2], [-8, WL], [-1, 4]], -32 * WL), 2 * B, ["ones"], ["hot2"])
-    for t in range(NT + 1):
-        ex_ = SETS[t]["m"] if t < NT else [0] * 10
-        mm([(T.pz[:, t * B:(t + 1) * B], ident(ex_[j]), T.hot[:, j * B:(j + 1) * B], j == 0, j == 9, B) for j in range(10)],
-           ["hot0", "hot1", "hot2"] + ["id%d" % m for m in ex_], ["pz"])
-    act(T.wgt[:], T.pz[:, 0:5 * B], ACT.Copy, 5 * B, (), ["pz", "wgt"])
-    for k, (va, vc) in enumerate(((-8.5, -1.0), (-11.5, -7.0), (3.5, -9.0))):
-        vec(lambda q, k=k, va=va: q.memset(T.tbi[:, k:k + 1], va), 1, (), ["tbi%d" % k])
-        vec(lambda q, k=k, vc=vc: q.memset(T.tbi[32 * WL:128, k:k + 1], vc), 1, (), ["tbi%d" % k])
-    vec(lambda q: q.memset(T.tiny[:], -2.0 ** -100), 4, (), ["tiny"])
-    vec(lambda q: q.tensor_copy(T.thb[0:8, :], T.thi[0:8, :]), 4, ["thi"], ["thb"])
-    mm([(T.pc[:, 0:4], T.bot[0:8, :], T.thb[0:8, :], True, True, 4)], ["bot", "thb"], ["pc"])
-    vec(ts(T.bth[:], T.pc[:, 0:4], -2.0, 21.0, ALU.mult, ALU.add), 4, (), ["pc", "bth"])
-    vec(lambda q: q.tensor_copy(T.off[:], T.ofi[:]), 4, ["ofi"], ["off"])
-    for t in range(1, NT):
-        vec(ts(T.ob[:, (t - 1) * W:t * W], T.zer[:, 0:W], T.off[:, t:t + 1], None, ALU.add), W, ["zer", "off"], ["ob%d" % t], 0.5)
-    gps(lambda q: q.iota(T.pi[:, 0:1], [[0, 1]], 0, 1), 1, (), ["pi"])
-    vec(ts(T.pa[:, 0:1], T.pi[:, 0:1], 15, None, ALU.bitwise_and), 1, ["pi"], ["pa"])
-    vec(ts(T.af[:, 0:1], T.pa[:, 0:1], 2.0, float(RAW), ALU.mult, ALU.add), 1, ["pa"], ["af"])
-    gps(lambda q: q.iota(T.l2[:], [[32, F // 16]], 0, 0, allow_small_or_imprecise_dtypes=True), F // 16, (), ["l2"])
-    gps(lambda q: q.iota(T.kr[:], [[2, SEG]], RAW - 32, 0, allow_small_or_imprecise_dtypes=True), SEG, (), ["kr"])
-    for h in range(4):
-        gps(lambda q, h=h: q.iota(T.io2[:, h * IW // 4:(h + 1) * IW // 4], [[2, IW // 4]], RAW + h * IW // 2, 0,
-                                  allow_small_or_imprecise_dtypes=True), IW // 4, (), ["io2_%d" % h])
-    gps(fill(T.low[:], NB * 2 * B, 2 * KH + RAW), NB * 2 * B, (), ["low%d" % j for j in range(NB)])
-    for j in range(NB):
-        act(T.low[:, (2 * j + 1) * B:(2 * j + 2) * B], T.l2[:, j * B:(j + 1) * B], ACT.Identity, B, ["l2", "af"], ["low%d" % j], bias=T.af[:, 0:1])
-    vec(ts(T.lo3[:, 0:3], T.low[:, B:B + 3], 1.0 / 4096, None, ALU.mult), 3, ["low0"], ["lo3"])
-    for b in range(3):
-        vec(ts(T.cst[:, b * SEG:(b + 1) * SEG - 1], T.kr[:, 0:SEG - 1], T.low[:, B + b:B + b + 1], T.lo3[:, b:b + 1], ALU.is_le, ALU.max), SEG,
-            ["kr", "low0", "lo3"], ["cst%d" % b])
-    gps(fill(T.cst[:, SEG - 1:3 * SEG:SEG], 3, 0), 3, (), ["cst3"])
-    gps(fill(T.eq[:], 3 * SEG, 2), 3 * SEG, (), ["eq%d" % k for k in range(8)])
-    for t in range(NT + 1):
-        gps(fill(inc[t][:, 0:IH], IH, 0), IH, (), ["inc%d" % t])
-    vec(lambda q: q.memset(T.slo[:], 0), NT * 2 * KH, (), ["slo%d" % t for t in range(NT)], 0.5)
+    def first():
+        gps(lambda q: q.iota(T.pi[:, 0:1], [[0, 1]], 0, 1), (), ["pi"])
+        fill(T.ones[:], 1.0, ["ones"])
+        blank(0)
+        sel(ident(0), 128, [[-1, 128]], 0, ["id0"])
+        scales = [2.0 ** m for m in range(10)] + [BIG, -BIG]
+        for k in (10, 11, 1, 2, 3, 4, 5, 6, 7, 8, 9):
+            act(ident(k), ident(0), ACT.Copy, ["id0"], ["id%d" % k], scale=scales[k])
 
-    def to_half(j, src, key):
-        for wl in range(WL):
-            vec(ts(T["xh%d" % j][:, wl:FB:WL], src[:, j * FB + 64 * wl:j * FB + 64 * wl + 64], -1024.0, None, ALU.add), 64, [key],
-                ["xh%d_%d" % (j, wl)])
+    def counts():
+        iota(T.l2[:], [[-32, F // 16]], 0, ["l2"])
+        iota(T.kr[:], [[-2, SEG]], RAW - 2 * C + 32, ["kr"])
 
-    for j in range(NB):
-        sl = slice(j * FB, (j + 1) * FB)
-        vec(ts(T.ta[:, sl], w2[0][:, sl], T.off[:, 0:1], None, ALU.add), FB, ["s0_%d" % j, "off"], ["ta%d" % j])
-        vec(ts(T.tb[:, sl], T.ta[:, sl], P - 1, None, ALU.bitwise_and), FB, ["ta%d" % j], ["tb%d" % j])
-        to_half(j, T.tb, "tb%d" % j)
+    def fills():
+        vec(ts(T.pa[:, 0:1], T.pi[:, 0:1], 15, None, ALU.bitwise_and), ["pi"], ["pa"])
+        fill(T.zer[:], 0.0, ["zer"])
+        vec(ts(T.af[:, 0:1], T.pa[:, 0:1], -2.0, RAW - 2.0 * C, ALU.mult, ALU.add), ["pa"], ["af"])
+        for k, v in enumerate((1e6, -1e6, RAW - 2.0 * C)):
+            fill(T.low[:, k:NB * 6 * B:3], v, ["low%d" % k])
+        for k, v in enumerate((-2.0 ** -100, -1.0, (P - 1 - RAW / 2.0) / 4096, -1024.0)):
+            fill(T.col[:, k:k + 1], v, ["col%d" % k])
+        fill(T.thx[:], 0.0, ["thx"])
+        fill(T.wgt[:, 6 * B * NT:6 * B * (NT + 2)], 0.0, ["wgt4"])
+        fill(T.cst[:, SEG - 1:3 * SEG:SEG], 0.0, ["cst3"])
+        for t in range(NT):
+            fill(T["slo%d" % t][:], 0, ["slo%d" % t])
 
-    upd = [None] * NT
-    fwd = [None] * (NT + 1)
+    def heads():
+        sfill(T.eq[:], 2.0, ["eq%d" % k for k in range(4)])
+        for t in range(NT + 1):
+            sfill(inc[t][:, C:IW], 0.0, ["inc%d" % t])
 
-    def front(t, j):
-        S = SETS[t]
-        k2 = (t * NB + j) % 2
-        pv, kv = T["pv%d" % k2], "pv%d" % k2
-        xh, lst, gb, gx, cmp_, pln = (T["%s%d" % (nm, j)] for nm in ("xh", "lst", "gb", "gx", "cmp", "pln"))
-        xk = ["xh%d_%d" % (j, wl) for wl in range(WL)]
-        if t == 0:
-            win, add_, pk = T.picw[:, HEAD:HEAD + P], 1024.0, ["pic0"]
-        else:
-            win, add_, pk = T.picw[:, 0:PW], 1024.0 + HEAD, ["pic0", "pic1", "pic2", "pic3"]
-        o = 0
-        for h, names in enumerate(SPLIT):
-            pl, kl, n = T["pl%d_%d" % (k2, h)], "pl%d_%d" % (k2, h), len(names)
-            if t == 0:
-                mm([(pl[:, s * W:(s + 1) * W], master(S[nm], u), xh[:, u * W:(u + 1) * W], u == 0, u == 3, W)
-                    for s, nm in enumerate(names) for u in range(4)], mkeys(t, names) + xk, [kl])
-            else:
-                mm([(pl[:, 0:n * W], T.zer[:, 0:128], T.zer[:, 0:n * W], True, False, n * W)] +
-                   [(pl[:, s * W:(s + 1) * W], master(S[nm], u), T.ob[:, (t - 1) * W:t * W], False, False, W)
-                    for s, nm in enumerate(names) for u in range(4)], mkeys(t, names) + ["zer", "ob%d" % t], [kl])
-                mm([(pl[:, s * W:(s + 1) * W], master(S[nm], u), xh[:, u * W:(u + 1) * W], False, s == n - 1 and u == 3, W)
-                    for s, nm in enumerate(names) for u in range(4)], mkeys(t, names) + xk, [kl])
-            vec(ts(lst[:, o * W:(o + n) * W], pl[:, 0:n * W], add_, None, ALU.add), n * W, (), [kl] + ["l%s%d" % (nm, j) for nm in names],
-                name="list%d%d" % (t, j))
-            o += n
-        at = {nm: k * W for k, nm in enumerate([x for names in SPLIT for x in names])}
-        WH, AH = W // HV, 16 // HV
-        for h in range(HV):
-            act(gb[:, 16 * WH * h:16 * WH * (h + 1)], win.indirect(lst[:, at["B"] + WH * h:at["B"] + WH * (h + 1)]), ACT.Copy, 16 * WH,
-                pk + ["lB%d" % j], ["gb%d_%d" % (j, h)], GAT, name="gB%d%d" % (t, j))
-        act(gx[:], win.indirect(lst[:, at["C"]:at["C"] + W]), ACT.Copy, 16 * W, pk + ["lC%d" % j], ["gx%d" % j], GAT, name="gC%d%d" % (t, j))
-        for h in range(HV):
-            for s, op, nm in ((0, ALU.is_gt, "A1"), (1, ALU.is_lt, "A2")):
-                vec(lambda q, s=s, op=op, h=h, nm=nm: q.tensor_tensor(cmp_[:, 32 * WH * h + s:32 * WH * (h + 1):2],
-                                                                      win.indirect(lst[:, at[nm] + WH * h:at[nm] + WH * (h + 1)]),
-                                                                      gb[:, 16 * WH * h:16 * WH * (h + 1)], op),
-                    16 * WH, pk + ["l%s%d" % (nm, j), "gb%d_%d" % (j, h)], ["ca%d_%d_%d" % (j, s, h)], GAT, name="A%d_%d%d" % (s, t, j))
-        mm([(pv[:, 128:128 + 8 * W], ident(10 + side), gx[:, side:16 * W:2], side == 0, side == 1, 8 * W) for side in range(2)],
-           ["id10", "id11", "gx%d" % j], [kv])
-        act(T["cmc%d" % j][:], pv[:, 128:128 + 8 * W], ACT.Sign, 8 * W, ["tiny"], [kv, "cc%d" % j], bias=T.tiny[:, 0:1],
-            name="sC%d%d" % (t, j))
-        mm([(pv[32 * WL:MV, a:128:16], T["cmc%d" % j][:, 8 * WL * a:8 * WL * (a + 1)], T.bo[:], True, True, -8 * WL) for a in range(16)],
-           ["bo", "cc%d" % j], [kv], name="vC%d%d" % (t, j))
-        for h in range(HV):
-            mm([(pv[0:32 * WL, a:128:16], cmp_[:, 32 * WL * a:32 * WL * (a + 1)], T.bo[:], True, True, 8) for a in range(AH * h, AH * (h + 1))],
-               ["bo", "ca%d_0_%d" % (j, h), "ca%d_1_%d" % (j, h)], [kv], name="votes%d%d" % (t, j))
-        for k in (1, 2, 0):
-            act(pln[0:MV, 128 * k:128 * k + 128], pv[0:MV, 0:128], ACT.Sign, 128, ["tbi%d" % k, kv], ["pln%d_%d" % (j, k)],
-                bias=T.tbi[0:MV, k:k + 1], scale=-1.0 if k == 2 else 1.0)
-        mm([(T.pc[:, 0:B], pln[0:MV, 128 * k:128 * k + 128], T.wgt[0:MV, 4 * B:5 * B], k == 1, k == 2, B) for k in (1, 2)],
-           ["wgt", "pln%d_1" % j, "pln%d_2" % j], ["pc"])
-        sg, yr, idx = T["sg%d" % j], T["yr%d" % j], T["idx%d" % j]
-        act(sg[:], T.pc[:, 0:B], ACT.Sign, B, ["bth"], ["pc", "sg%d" % j], bias=T.bth[:, t:t + 1], name="sg%d%d" % (t, j))
-        mm([x for h in range(2) for x in ((T.pz[:, h * B:(h + 1) * B], pln[0:MV, 0:128], T.wgt[0:MV, t * B:(t + 1) * B], True, False, B),
-                                          (T.pz[:, h * B:(h + 1) * B], ident(10 + 2 * h), sg[:], False, True, B))],
-           ["wgt", "pln%d_0" % j, "sg%d" % j, "id10", "id12"], ["pz"])
-        vec(lambda q: q.tensor_tensor(yr[:], T.pz[:, 0:2 * B], T.low[:, 2 * j * B:(2 * j + 2) * B], ALU.max), 2 * B, ["low%d" % j],
-            ["pz", "yr%d" % j])
-        vec(ts(idx[:], yr[:], 0.5, -RAW / 2.0, ALU.mult, ALU.add), 2 * B, ["yr%d" % j], ["idx%d" % j], name="idx%d%d" % (t, j))
+    def floors():
+        for j in range(NB):
+            vec(ts(T.low[:, (6 * j + 3) * B + 2:(6 * j + 6) * B:3], T.l2[:, j * B:(j + 1) * B], T.af[:, 0:1], None, ALU.add), ["l2", "af", "low2"],
+                ["lowb%d" % j])
+        o = 3 * B + 2
+        vec(ts(T.own[:, 0:3], T.low[:, o:o + 9:3], 2.0 * (P - 1 - SP + C) - RAW, 1.0 / 8192, ALU.add, ALU.mult), ["lowb0"], ["lo3"])
 
-    def back(t, j):
-        idx, ga = T["idx%d" % j], T["ga%d" % j]
-        sl = slice(j * FB, (j + 1) * FB)
-        aft = [(first, T_BANK0)] if t == 0 else []
-        act(ga[:], inc[t][:, 0:IW].indirect(idx[:, 0:B]), ACT.Copy, FB, ["idx%d" % j, "inc%d" % t], ["ga%d" % j], GAT,
-            ext=[arr_inc(0)] if t == 0 else [], after=aft, name="g1_%d%d" % (t, j))
-        out, ko = (w2[t + 1][:, sl], "s%d_%d" % (t + 1, j)) if t < NT - 1 else (T.ta[:, sl], "ta%d" % j)
-        vec(lambda q: q.tensor_tensor(out, w2[t][:, 0:F + C].indirect(idx[:, B:2 * B]), ga[:], ALU.add), FB,
-            ["idx%d" % j, "ga%d" % j] + ["s%d_%d" % (t, k) for k in range(NB)], [ko], GAT, ext=[arr_ex(t)], after=aft, name="new%d%d" % (t, j))
-        if t < NT - 1:
-            to_half(j, w2[t + 1], ko)
-        else:
-            vec(ts(T.tb[:, sl], out, P - 1, None, ALU.bitwise_and), FB, [ko], ["tb%d" % j])
-            vec(lambda q: q.tensor_copy(T.ysf[:, sl], T.tb[:, sl]), FB, ["tb%d" % j], ["ysf%d" % j])
-            dma("y", T.ys[:, sl], T.ysf[:, sl], 2.5, ["ysf%d" % j], ())
+    def cst():
+        o = 3 * B + 2
+        for b in range(3):
+            vec(ts(T.cst[:, b * SEG:(b + 1) * SEG - 1], T.kr[:, 0:SEG - 1], T.low[:, o + 3 * b:o + 3 * b + 1], T.own[:, b:b + 1], ALU.is_ge, ALU.max),
+                ["kr", "lowb0", "lo3"], ["cst%d" % b])
 
-    def halve(t):
-        pieces, c = [], 3 * t
-        while c < 3 * t + 3:
-            j = c // B
-            e = min(3 * t + 3, (j + 1) * B)
-            pieces.append((j, c - j * B, e - c, c - 3 * t))
-            c = e
-        ik = ["io2_%d" % h for h in range(4)]
-        for pn, (j, c0, nc, pos) in enumerate(pieces):
-            odd = c0 % 2
-            act(T.eq[:, SEG * pos + SEG - 1:SEG * (pos + nc):SEG], T["yr%d" % j][:, c0:c0 + nc], ACT.Copy, nc, ["yr%d" % j], ["eq%d" % (6 + pn)],
-                scale=1.0 / 4096)
-            vec(ts(T["hvo%d" % t][:, 16 * pos:16 * (pos + nc)], T["ga%d" % j][:, 16 * c0:16 * (c0 + nc)], 0.5, -0.25, ALU.mult, ALU.add),
-                16 * nc, ["ga%d" % j], ["hvo%d" % t])
-            for b in range(3):
-                jb, cb = (3 * t + b) // B, (3 * t + b) % B
-                a = SEG * b + 16 + 16 * (pos - odd)
-                act(T.eq[:, a:a + 16 * (nc + odd)], T.io2[:, 0:IW].indirect(T["idx%d" % j][:, c0 - odd:c0 + nc]), ACT.Abs, 16 * (nc + odd),
-                    ik + ["idx%d" % j, "yr%d" % jb], ["eq%d" % (2 * b + pn)], GAT, bias=T["yr%d" % jb][:, cb:cb + 1], scale=-1.0)
-        vec(lambda q: q.tensor_tensor_scan(T.sc[:], T.eq[:], T.cst[:], 1.0, ALU.min, ALU.max), 3 * SEG,
-            ["eq%d" % k for k in range(8)] + ["cst0", "cst1", "cst2", "cst3"], ["sc"])
-        vec(ts(slo(t, 3), T.sc[:, SEG - 1:3 * SEG:SEG], 2048.0, -RAW / 2.0, ALU.mult, ALU.add), 3, ["sc"], ["slo%d" % t])
+    def bos():
+        sel(T.bot[0:8, :], 128, [[1, 8], [0, 16]], 0, ["bot"], cm=-1, parts=8)
+        mm(group([(T.pz0[:, 0:8], T.bot[0:8, :], T.idn[0:8, 0:8])]), ["bot", "id0"], ["pz0"])
+        for k, a in enumerate((15 / 128, 11 / 128, 5 / 16, 1.0, 73 / 512, -7 / 64)):
+            act(T.bos[:, 8 * k:8 * k + 8], T.pz0[:, 0:8], ACT.Copy, ["pz0"], ["bos%d" % k], scale=a)
+
+    def off():
+        vec(lambda q: q.tensor_copy(T.off[:], T.ofi[:]), ["ofi"], ["off"])
+
+    def thr():
+        vec(ts(T.thx[0:8, MV - MA:MV - MA + NT], T.thi[0:8, :], -2.0, 21.0, ALU.mult, ALU.add), ["thi"], ["thx"])
+
+    def rows():
+        mm(group([(T.pz0[MA:128, 0:128], T.thx[0:8, :], T.bot[0:8, :])]), ["bot", "thx"], ["pz0"])
+        for j in range(NB):
+            vec(lambda q: q.tensor_copy(T["pln%d" % j][MA:128, 0:128], T.pz0[MA:128, 0:128]), ["pz0"], ["pln%d" % j])
+
+    def hot():
+        for s in range(2):
+            sel(T.hot[:, 8 * B * s:8 * B * (s + 1)], 8 * B, [[-2 * B, 4], [0, 2], [-2, B]], -s, ["hot%d" % s])
+        sel(T.hot[:, 16 * B:20 * B], 4 * B, [[-B, 2], [0, 2], [-1, B]], -MA, ["hot2"])
+        sel(T.hot[:, 20 * B:24 * B], 4 * B, [[-1, 4], [0, B]], -MV, ["hot3"])
+
+    def hots(k, n=1):
+        return T.hot[:, 2 * k * B:(2 * k + n) * B]
+
+    def wgt(k, rows_=128):
+        return T.wgt[0:rows_, 6 * B * k:6 * B * (k + 1)]
+
+    def third(tile, o, part, k):
+        return tile[:, o + 3 * B * part + k:o + 3 * B * (part + 1):3]
+
+    def wc():
+        mm(group([(T.pz1[:, 0:B], ident(10), hots(k)) for k in range(10)]) + group([(T.pz1[:, B:2 * B], ident(11 if k < 8 else 10), hots(k)) for k in range(10)]),
+           ["hot0", "hot1", "hot2", "id10", "id11"], ["pz1"])
+
+    def wd():
+        for k in range(2):
+            for part in range(2):
+                vec(ts(third(T.wgt, 6 * B * (NT + k), part, 1), T.pz1[:, k * B:(k + 1) * B], 1.0 - 2 * part, None, ALU.mult), ["pz1", "wgt4"],
+                    ["wd%d" % (2 * k + part)])
+
+    def weights(ts_, kb):
+        for t in ts_:
+            o = 6 * B * (t - ts_[0])
+            mm(group([(T[kb][:, o:o + 6 * B], T.zer[:, 0:128], T.zer[:, 0:6 * B])]
+                     + [(T[kb][:, o + 2:o + 6 * B:3], ident(SETS[t]["m"][k]), hots(k, 2)) for k in range(10)]
+                     + [(third(T[kb], o, part, 1), ident(11 - part), T.hot[:, (20 + t) * B:(21 + t) * B]) for part in range(2)]),
+               ["zer", "hot0", "hot1", "hot2", "hot3"] + ["id%d" % m for m in range(12)], [kb])
+
+    def keep_weights(ts_, kb):
+        act(T.wgt[:, 6 * B * ts_[0]:6 * B * (ts_[-1] + 1)], T[kb][:, 0:6 * B * len(ts_)], ACT.Copy, [kb], ["wgt%d" % t for t in ts_], scale=-1.0)
+
+    def ob():
+        for t in range(1, NT):
+            vec(ts(T.ob[:, (t - 1) * W:t * W], T.zer[:, 0:W], T.off[:, t:t + 1], None, ALU.add), ["zer", "off"], ["ob%d" % t])
+
+    def spread(t, kb, o):
+        for s, nm in enumerate(NAMES):
+            mm(group([(T[kb][:, o + s * W:o + (s + 1) * W], master(SETS[t][nm], u), T.ob[:, (t - 1) * W:t * W]) for u in range(4)]),
+               mkeys(t, [nm]) + ["ob%d" % t], [kb])
+
+    def keep_spread(ts_, kb):
+        vec(lambda q: q.tensor_copy(T.obl[:, 4 * W * (ts_[0] - 1):4 * W * ts_[-1]], T[kb][:, 0:4 * W * len(ts_)]), [kb], ["obl%d" % t for t in ts_])
+
+    def io2():
+        for h in range(2):
+            iota(T.io2[:, h * IW // 2:(h + 1) * IW // 2], [[-2, IW // 2]], RAW - h * IW, ["io2_%d" % h])
+
+    def prep():
+        for k in range(NB + 2):
+            for step, j in ((0, k), (1, k - 1), (2, k - 2)):
+                sl = slice(j * FB, (j + 1) * FB)
+                if not 0 <= j < NB:
+                    continue
+                if step == 0:
+                    vec(ts(T.ta[:, sl], w2[0][:, C + j * FB:C + (j + 1) * FB], T.off[:, 0:1], None, ALU.add), ["s0_%d" % j, "off"], ["ta%d" % j])
+                elif step == 1:
+                    vec(ts(T.tb[:, sl], T.ta[:, sl], P - 1, None, ALU.bitwise_and), ["ta%d" % j], ["tb%d" % j])
+                else:
+                    vec(ts(T["xh%d" % j][:], T.tb[:, sl], -1024.0, None, ALU.add), ["tb%d" % j], ["xh%d" % j])
 
     def apply_update(t):
-        aft = [(upd[t], T_UPD)] + ([(fwd[t + 1], T_FWD)] if fwd[t + 1] is not None else [])
-        vec(lambda q: q.tensor_copy(inc[t + 1][:, 0:IW].indirect(T["sli%d" % t][:, 0:3]), T["hvi%d" % t][:]), KH, (), ["inc%d" % (t + 1)], SCA,
-            ext=[arr_upd(t), arr_inc(t + 1)], after=aft, name="apply%d" % t)
+        vec(lambda q: q.tensor_copy(inc[t + 1][:, 0:IW].indirect(T["sli%d" % t][:, 0:3]), T["hvi%d" % t][:]), (), ["inc%d" % (t + 1)],
+            ext=[arr_upd(t), arr_inc(t + 1)])
+        if t < NT - 1:
+            send(ring(t + 1), inc[t + 2][:, 0:C], inc[t + 1][:, 0:C], "ai%d" % (t + 2), ["inc%d" % (t + 1)])
+        else:
+            dma("s", T.yi[:], inc[NT][:, 0:C], ["inc%d" % NT], ())
 
-    jh = [(3 * t + 2) // B for t in range(NT)]
-    for t in range(NT):
-        dst = (rank - 1) % N if t < NT - 1 else (rank + NT) % N
-        if t >= 1:
-            fwd[t + 1] = send(10 + t, dst, inc[t + 1][:, IH:IW], inc[t][:, IH:IW], "ai%d" % (t + 1), ["inc%d" % t])
-        for j in range(NB):
-            front(t, j)
-        for j in range(NB):
-            back(t, j)
-            if j == jh[t]:
-                halve(t)
-                if t == 0 and handed_on(r0, 1):
-                    send(5, r0, inc[1][:, IH:IW], inc[0][:, IH:IW], "ai1", ["inc0"], ext=[arr_inc(0)], after=[(first, T_BANK0)])
-                    send(6, r0, w2[1][:, F:F + C], w2[0][:, F:F + C], "ae1", (), ext=[arr_ex(0)])
-                upd[t] = send_update(20 + t, dst, t)
-                if t == 0:
-                    late = [tt for tt in (2, 3) if not handed_on((rank - 1 - tt) % N, tt)]
-                    for k, tt in enumerate(late):
-                        send(7 + k, (rank - 1 - tt) % N, w2[tt][:, F:F + C], T.exo[:], "ae%d" % tt, ["exo0", "exo1"])
-                if t in (0, 1) and handed_on(r0, t + 2):
-                    send(30 + t, r0, w2[t + 2][:, F:F + C], w2[t + 1][:, F:F + C], "ae%d" % (t + 2), (), ext=[arr_ex(t + 1)])
-        apply_update(t)
-    dma("y", T.yi[:], inc[NT][:, IH:IW], 2.8, ["inc%d" % NT], ())
+    once = dict(loads=loads, first=first, counts=counts, floors=floors, cst=cst, off=off, bos=bos, fills=fills, thr=thr, rows=rows, hot=hot, wc=wc, wd=wd,
+                prep=prep, ob=ob, io2=io2, go=go, copies=copies, bank1=bank1, hand1=lambda: hand_on(1), last=lambda: apply_update(NT - 1),
+                heads=heads, w0=lambda: weights([0], "pd"), w0c=lambda: keep_weights([0], "pd"))
+    for k in range(1, NT):
+        once.update({"w%d" % k: lambda k=k: weights([k], "pw"), "w%dc" % k: lambda k=k: keep_weights([k], "pw"),
+                     "o%d" % k: lambda k=k: spread(k, "pw", 0), "o%dc" % k: lambda k=k: keep_spread([k], "pw")})
+    for k in range(NT):
+        once["m%d" % k] = lambda k=k: masters(k)
+        once["z%d" % k] = lambda k=k: blank(k)
+        once["pc%d" % k] = lambda k=k: PICV[k] == "y" or again(k)
+        once["b%d" % k] = lambda k=k: bank0(k)
 
-    order = call_order(nodes)
-    INFO[rank] = (nodes, order)
-    counts, waited = {}, {}
-    for i in order:
-        nd = nodes[i]
-        q, e = Q[nd["eng"]], nd["eng"]
-        need = {}
-        for p in nd["dep"]:
-            need[nodes[p]["sem"]] = max(need.get(nodes[p]["sem"], 0), nodes[p]["val"])
-        for s, v in nd["ext"]:
-            need[s] = max(need.get(s, 0), v)
-            totals[s] = max(totals.get(s, 0), v)
-        for s in sorted(need):
-            if waited.get((e, s), 0) < need[s]:
-                q.wait_ge(T.sem[s], int(need[s]))
-                waited[(e, s)] = need[s]
-        ins = nd["fn"](q)
-        if nd["kind"] == "d":
-            ins[0].then_inc(T.sem[nd["sem"]], 16)
-            nd["val"] = totals[nd["sem"]] = 16
-        elif nd["kind"] == "c":
-            nd["sem"] = QSEM[e]
-            for x in ins:
-                x.then_inc(T.sem[nd["sem"]], 1)
-            nd["val"] = counts[nd["sem"]] = counts.get(nd["sem"], 0) + len(ins)
-    totals.update(counts)
+    def batch(n):
+        t, j = divmod(n, NB)
+        S = SETS[t]
+        pv, pd, pz, kv, kz = T["pv%d" % j], T.pd, T["pz%d" % j], "pv%d" % j, "pz%d" % j
+        xh, lst, gb, gx, cmp_, cmc, pln, yr, idx, ga = (T["%s%d" % (nm, j)] for nm in ("xh", "lst", "gb", "gx", "cmp", "cmc", "pln", "yr", "idx", "ga"))
+        if t == 0:
+            win, pk = T.picw[:, HEAD:HEAD + P], ["pic0"]
+        else:
+            win = T.picw[:, HEAD - STEP * t:HEAD + 2 * P + STEP * t]
+            pk = ["pic0", "pic2", "pic3"] + ["pic1_%d" % k for k in range(4)] + (["pic4", "pic5"] if t > 1 else [])
+        sl = slice(j * FB, (j + 1) * FB)
+        do = {}
+
+        def lists(h, o, names, offsets):
+            pl, kl, k = T["pl%d" % h], "pl%d" % h, len(names)
+            picks = [(pl[:, s * W:(s + 1) * W], master(S[nm], u), xh[:, u:FB:4] if nm == "C" else xh[:, u * W:(u + 1) * W])
+                     for s, nm in enumerate(names) for u in range(4)]
+            if t == 0:
+                if not offsets:
+                    mm([x for s in range(k) for x in group(picks[4 * s:4 * s + 4])], mkeys(t, names) + ["xh%d" % j], [kl])
+                return
+            c0 = 4 * W * (t - 1) + o * W
+            both = group([(pl[:, 0:k * W], ident(0), T.obl[:, c0:c0 + k * W])] + picks)
+            if offsets:
+                mm(both[:1], ["id0", "obl%d" % t], [kl])
+            else:
+                mm(both[1:], mkeys(t, names) + ["xh%d" % j], [kl])
+
+        def convert(h, o, names):
+            k = len(names)
+            vec(ts(lst[:, o * W:(o + k) * W], T["pl%d" % h][:, 0:k * W], 1024.0 + STEP * t, None, ALU.add), ["pl%d" % h],
+                ["l%s%d" % (nm, j) for nm in names])
+
+        for h, (nm, o, names) in enumerate((("B", 0, NAMES[:1]), ("R", 1, NAMES[1:]))):
+            do["O" + nm] = lambda h=h, o=o, names=names: lists(h, o, names, True)
+            do["L" + nm] = lambda h=h, o=o, names=names: lists(h, o, names, False)
+            do["list" + nm] = lambda h=h, o=o, names=names: convert(h, o, names)
+
+        def pixels(nm, a, b):
+            o = NAMES.index(nm) * W
+            return win.indirect(lst[:, o + a:o + b])
+
+        for h, (a, b) in enumerate(zip(BCUTS, BCUTS[1:])):
+            do["gB%d" % h] = lambda a=a, b=b: act(gb[:, 16 * a:16 * b], pixels("B", a, b), ACT.Copy, pk + ["lB%d" % j],
+                                                  ["gb%d_%d" % (j, k) for k in range(a // 8, b // 8)])
+        for h, (a, b) in enumerate(zip(CUTS, CUTS[1:])):
+            for s, op, nm in ((0, ALU.is_gt, "A1"), (1, ALU.is_lt, "A2")):
+                o = MA * (a % 16) + 2 * (a // 16) + s
+                dst = cmp_[:, 32 * a + s:32 * b:2] if MODE == "wl" else cmp_[:, o:o + MA * (b - a) - 2 * WL + 1:2 * WL]
+                do["a%d" % (2 * h + s)] = lambda a=a, b=b, s=s, op=op, nm=nm, dst=dst: vec(
+                    lambda q: q.tensor_tensor(dst, pixels(nm, a, b), gb[:, 16 * a:16 * b], op),
+                    pk + ["l%s%d" % (nm, j)] + ["gb%d_%d" % (j, k) for k in range(a // 8, b // 8)],
+                    ["ca%d_%d_%d" % (j, s, k) for k in range(a // 8, b // 8)])
+            if n >= XP and h == WL - 1:
+                keys = ["gb%d_%d" % (j, k) for k in range(a // 8, b // 8)]
+                do["gX"] = lambda a=a, b=b: act(T.gs[:], pixels("A2", a, b), ACT.Copy, pk + ["lA2%d" % j], ["gs"])
+                do["pX"] = lambda a=a, b=b, keys=keys: mm(group([(T.pz1[:, 0:256], ident(0), gb[:, 16 * a:16 * b])]), ["id0"] + keys, ["pz1"])
+                do["a5"] = lambda a=a, b=b, dst=dst: vec(lambda q: q.tensor_tensor(dst, T.gs[:], T.pz1[:, 0:256], ALU.is_lt), ["gs", "pz1"],
+                                                         ["ca%d_1_%d" % (j, k) for k in range(a // 8, b // 8)])
+            if MODE == "wl":
+                do["vA%d" % h] = lambda a=a, b=b: mm(
+                    [(pv[32 * (w // 16):32 * (w // 16) + 32, w % 16:384:16], cmp_[:, 32 * w:32 * w + 32], T.bos[:, 0:24], True, True) for w in range(a, b)],
+                    ["bos0", "bos1", "bos2"] + ["ca%d_%d_%d" % (j, s, k) for s in range(2) for k in range(a // 8, b // 8)], [kv])
+        if MODE != "wl":
+            do["vA0"] = lambda: mm([(pv[0:MA, a:384:16], cmp_[:, MA * a:MA * (a + 1)], T.bos[:, 0:24], True, True) for a in range(16)],
+                                   ["bos0", "bos1", "bos2"] + ["ca%d_%d_%d" % (j, s, k) for s in range(2) for k in range(2 * WL)], [kv])
+        for h, (a, b) in enumerate(zip(CCUTS, CCUTS[1:])):
+            do["gC%d" % h] = lambda h=h, a=a, b=b: act(gx[:, 16 * a:16 * b], pixels("C", a, b), ACT.Copy, pk + ["lC%d" % j], ["gx%d_%d" % (j, h)])
+        do["D"] = lambda: mm([x for pair in range(2) for x in group([(pd[:, pair * FB:(pair + 1) * FB], ident(10 + side), gx[:, 2 * pair + side:4 * FB:4])
+                                                                    for side in range(2)])],
+                             ["id10", "id11"] + ["gx%d_%d" % (j, h) for h in range(len(CCUTS) - 1)], ["pd"])
+        do["sC"] = lambda: act(cmc[:], pd[:, 0:2 * FB], ACT.Sign, ["pd", "col0"], ["cc%d" % j], bias=T.col[:, 0:1])
+        do["vC0"] = lambda: mm([(pv[MA:MV, a:384:16], cmc[:, a:2 * FB:16], T.bos[:, 24:48], True, True) for a in range(16)],
+                               ["bos3", "bos4", "bos5", "cc%d" % j], [kv])
+        do["pln0"] = lambda: act(pln[0:MV, :], pv[0:MV, 0:384], ACT.Sign, [kv, "col1"], ["pln%d" % j], bias=T.col[0:MV, 1:2])
+        do["Z"] = lambda: mm(group([(pz[:, 0:6 * B], pln[:, 0:128], wgt(t))] +
+                                   [(pz[:, 0:6 * B], pln[0:MV, 128 * k:128 * k + 128], wgt(NT - 1 + k, MV)) for k in (1, 2)]),
+                             ["wgt%d" % t, "pln%d" % j] + ["wd%d" % k for k in range(4)], [kz])
+        do["yr"] = lambda: vec(lambda q: q.tensor_tensor_scan(yr[:], pz[:, 0:6 * B], T.low[:, 6 * B * j:6 * B * (j + 1)], 0.0, ALU.min, ALU.max),
+                               ["low0", "low1", "low2", "lowb%d" % j, kz], ["yr%d" % j])
+        do["idx"] = lambda: vec(ts(idx[:], yr[:, 2:6 * B:3], -0.5, RAW / 2.0, ALU.mult, ALU.add), ["yr%d" % j], ["idx%d" % j])
+        do["ga"] = lambda: act(ga[:], inc[t][:, 0:IW].indirect(idx[:, 0:B]), ACT.Identity, ["idx%d" % j, "inc%d" % t, "col3"], ["ga%d" % j],
+                               bias=T.col[:, 3:4] if t < NT - 1 else 0.0, ext=[arr_inc(0)] if t == 0 else [])
+        out, ko = (xh[:], "xh%d" % j) if t < NT - 1 else (T.ta[:, sl], "ta%d" % j)
+        do["new"] = lambda: vec(lambda q: q.tensor_tensor(out, w2[t][:, 0:C + F].indirect(idx[:, B:2 * B]), ga[:], ALU.add),
+                                ["idx%d" % j, "ga%d" % j] + ["s%d_%d" % (t, k) for k in range(NB)], [ko], ext=[arr_ex(t)])
+
+        def store():
+            vec(lambda q: q.tensor_copy(T.ysf[:, sl], T.tb[:, sl]), ["tb%d" % j], ["ysf%d" % j])
+            dma("y", T.ys[:, sl], T.ysf[:, sl], ["ysf%d" % j], ())
+
+        if t < NT - 1:
+            do["half"] = lambda: vec(ts(w2[t + 1][:, C + j * FB:C + (j + 1) * FB], xh[:], 1024.0, None, ALU.add), [ko], ["s%d_%d" % (t + 1, j)])
+        else:
+            do["half"] = lambda: vec(ts(T.tb[:, sl], out, P - 1, None, ALU.bitwise_and), [ko], ["tb%d" % j])
+            do["store"] = store
+        if j:
+            return do
+
+        c0, odd = 3 * t, 3 * t % 2
+        msg = T["hvo%d" % t]
+
+        def eq():
+            for b in range(3):
+                act(T.eq[:, SEG * b + 16 - 16 * odd:SEG * b + 64], T.io2[:, 0:IW].indirect(idx[:, c0 - odd:c0 + 3]), ACT.Abs,
+                    ["io2_0", "io2_1", "idx0", "yr0"], ["eq%d" % b], bias=yr[:, 3 * (c0 + b) + 2:3 * (c0 + b) + 3], scale=-1.0)
+            act(T.eq[:, SEG - 1:3 * SEG:SEG], yr[:, 3 * c0 + 2:3 * (c0 + 3):3], ACT.Identity, ["yr0", "col2"], ["eq3"], scale=1.0 / 8192,
+                bias=T.col[:, 2:3])
+
+        def update():
+            vec(ts(T["slo%d" % t][:, 0:3], T.sc[:, SEG - 1:3 * SEG:SEG], -4096.0, P - 1.0, ALU.mult, ALU.add), ["sc"], ["slo%d" % t])
+            es = engines(core, ring(t))
+            rid, pid = topo.addr(ring(t), core)
+            h = len(es) // 2
+            totals["sent"] += len(es)
+            tr = [RemoteDMATransfer(dst_ids=[DstId(rid=rid, pnc=pid)], dma_engine_mask=bits(e), remote_sem=T.sem["au%d" % t], src=a, dst=b)
+                  for e, a, b in ((es[:h], T["slo%d" % t][:], T["sli%d" % t][:]), (es[h:], msg[:], T["hvi%d" % t][:]))]
+            add("g", lambda q: q.remote_dma_fused(tr, local_sem=T.sem.sent), ["slo%d" % t, "hvo%d" % t], (), kind="r")
+            for k in range(2, NT):
+                if t == 0 and not handed_on((rank - 1 - k) % N, k):
+                    send(cores[(rank - 1 - k) % N], w2[k][:, 0:C], T.exo[:], "ae%d" % k, ["own1", "own2"])
+            if t + 2 < NT:
+                hand_on(t + 2)
+
+        do["eq"] = eq
+        do["hvo"] = lambda: vec(ts(msg[:, 0:KH], ga[:, 16 * c0:16 * c0 + KH], 0.5, 511.75 if t < NT - 1 else -0.25, ALU.mult, ALU.add),
+                                ["ga0"], ["hvo%d" % t])
+        do["scan"] = lambda: vec(lambda q: q.tensor_tensor_scan(T.sc[:], T.eq[:], T.cst[:], 1.0, ALU.min, ALU.max),
+                                 ["eq%d" % k for k in range(4)] + ["cst%d" % k for k in range(4)], ["sc"])
+        do["slo"] = update
+        if t:
+            do["apply"] = lambda: apply_update(t - 1)
+        return do
+
+    batches = [batch(n) for n in range(NT * NB)]
+
+    def run(order, n):
+        for name in order.split():
+            m = n + name.count("+") - name.count("-")
+            nm = name.rstrip("+-")
+            if nm[:3] == "job":
+                nm = JOBS[m] + nm[3:] if m in JOBS else ""
+            if nm in once:
+                once.pop(nm)()
+            elif 0 <= m < len(batches) and nm in batches[m]:
+                batches[m].pop(nm)()
+
+    run(START, 0)
+    for n in range(-2, NT * NB + 3):
+        run(OTHER.get(n, SLOT), n)
+    run("last", 0)
     for s in sorted(totals):
         if max([v for (e, k), v in waited.items() if k == s] + [0]) < totals[s]:
             g.wait_ge(T.sem[s], int(totals[s]))

from concourse.bass import DstId, RemoteDMATransfer
from concourse.mybir import AluOpType, ActivationFunctionType

ALU = AluOpType
ACT = ActivationFunctionType

P, F, C, NT, KH, D0 = 2048, 384, 1024, 4, 48, 6
MODE = "six"
PICV = "yyyy"
GO = 1
XP = 99
LOADS = "isep"
WIDE0 = 1
NB = 2
FB = F // NB
W = FB // 4
B = FB // 16
WL = FB // 64
MA = 8 * B
MV = 10 * B
NAMES = ("B", "A1", "A2", "C")
STEP = 256
HEAD = STEP * (NT - 1)
PW = 2 * P + 2 * HEAD
SP = C + 16
IW = SP + KH
MW = 144
RAW = C - 1
BIG = 2048.0
SEG = 65

SETS = []
for _t in range(NT):
    _d = D0 - _t
    _x = 5 if _d == 3 else 2
    _m = [_b0 + _x * (_k >> 1) + (_k & 1) for _b0 in (0, _d) for _k in range(4)]
    _rest = sorted(set(range(10)) - set(_m))
    SETS.append({"B": (_d, _x), "A1": (0, _x), "A2": (2 * _d, _x), "C": (_rest[0], _rest[1] - _rest[0], _d), "m": _m + _rest})
MASTERS = []
for _t in range(NT):
    for _n in NAMES:
        if SETS[_t][_n] not in MASTERS:
            MASTERS.append(SETS[_t][_n])
NM = len(MASTERS)

SCRATCH = {
    "picw": ("sbuf", [128, PW], "bfloat16"),
    "exo": ("sbuf", [128, C], "int32"),
    "inco": ("sbuf", [128, C], "bfloat16"),
    "ofi": ("sbuf", [128, 4], "int32"),
    "off": ("sbuf", [128, 4], "float32"),
    "thi": ("sbuf", [128, 4], "int32"),
    "thx": ("sbuf", [128, 128 - MA], "bfloat16"),
    "ob": ("sbuf", [128, 3 * W], "float16"),
    "obl": ("sbuf", [128, 12 * W], "float16"),
    "ta": ("sbuf", [128, F], "int32"),
    "tb": ("sbuf", [128, F], "int32"),
    "ysf": ("sbuf", [128, F], "float32"),
    "mst": ("sbuf", [128, NM * MW], "bfloat16"),
    "ones": ("sbuf", [128, 128], "bfloat16"),
    "zer": ("sbuf", [128, 128], "bfloat16"),
    "idn": ("sbuf", [128, 12 * 128], "bfloat16"),
    "bos": ("sbuf", [128, 48], "bfloat16"),
    "bot": ("sbuf", [128, 128], "bfloat16"),
    "hot": ("sbuf", [128, 24 * B], "bfloat16"),
    "wgt": ("sbuf", [128, 36 * B], "bfloat16"),
    "gs": ("sbuf", [128, 256], "bfloat16"),
    "col": ("sbuf", [128, 8], "float32"),
    "pi": ("sbuf", [128, 4], "int32"),
    "pa": ("sbuf", [128, 4], "int32"),
    "af": ("sbuf", [128, 4], "float32"),
    "l2": ("sbuf", [128, F // 16], "float32"),
    "low": ("sbuf", [128, NB * 6 * B], "float32"),
    "own": ("sbuf", [128, 4], "float32"),
    "kr": ("sbuf", [128, SEG], "float32"),
    "cst": ("sbuf", [128, 3 * SEG], "float32"),
    "eq": ("sbuf", [128, 3 * SEG], "float32"),
    "sc": ("sbuf", [128, 3 * SEG], "float32"),
    "io2": ("sbuf", [128, IW], "float32"),
}
for _n in ("pl0", "pl1", "pv0", "pv1", "pd", "pw", "pz0", "pz1"):
    SCRATCH[_n] = ("psum", [128, 512], "float32")
for _t in range(NT):
    SCRATCH["w2_%d" % _t] = ("sbuf", [128, C + F], "int32")
    SCRATCH["slo%d" % _t] = ("sbuf", [128, 2 * KH], "uint16")
    SCRATCH["sli%d" % _t] = ("sbuf", [128, 2 * KH], "uint16")
    SCRATCH["hvo%d" % _t] = ("sbuf", [128, KH], "int32")
    SCRATCH["hvi%d" % _t] = ("sbuf", [128, KH], "int32")
for _t in range(NT + 1):
    SCRATCH["inc%d" % _t] = ("sbuf", [128, IW], "bfloat16")
for _j in range(NB):
    SCRATCH["xh%d" % _j] = ("sbuf", [128, FB], "float16")
    SCRATCH["lst%d" % _j] = ("sbuf", [128, 4 * W], "uint16")
    SCRATCH["gb%d" % _j] = ("sbuf", [128, 16 * W], "bfloat16")
    SCRATCH["gx%d" % _j] = ("sbuf", [128, 16 * W], "bfloat16")
    SCRATCH["cmp%d" % _j] = ("sbuf", [128, 32 * W], "bfloat16")
    SCRATCH["cmc%d" % _j] = ("sbuf", [128, 8 * W], "bfloat16")
    SCRATCH["pln%d" % _j] = ("sbuf", [128, 3 * 128], "bfloat16")
    SCRATCH["yr%d" % _j] = ("sbuf", [128, 6 * B], "float32")
    SCRATCH["idx%d" % _j] = ("sbuf", [128, 2 * B], "uint16")
    SCRATCH["ga%d" % _j] = ("sbuf", [128, FB], "float32")

SEMAPHORES = (["qv", "qs", "qp", "qg", "sent", "go"] + ["d%d" % i for i in range(20)] + ["ae%d" % t for t in range(NT)]
              + ["ai%d" % t for t in range(NT + 1)] + ["au%d" % t for t in range(NT)])

CUTS = (0, 16, 32, 48)
BCUTS = (0, 16, 32, 48)
CCUTS = (0, 16, 48)
START = "loads first m0 fills z1 off heads z2 z3 prep b0 b1 b2 go counts hot"
SLOT = "a1 hvo-- gB1 slo-- a0 OB+ vC0- pln0- a2 Z- gB2 half-- OR+ yr- job apply- gC0 idx- a4 ga- store-- new- a5 gC1 LB+ eq- listB+ LR+ D gB0+ a3 listR+ scan- sC vA0 jobc"
OTHER = {-1: "LB+ LR+ listB+ ob thr gB0+ listR+ LB++ gB1+ listB++ gB2+ LR++ floors cst copies wc w0", 0: "gC1 a0 a3 gC0 bos m1 bank1 io2 m2 hand1 m3 listR+ a1 a2 gB0+ w0c D rows gB1+ a5 sC a4 wd vA0", 1: "a3 vC0- a0 gC0 a1 o1 pln0- Z- o1c gB2 yr- idx- job a2 OB+ ga- OR+ new- LB+ eq- listB+ gC1 a5 LR+ gB0+ listR+ jobc D a4 sC scan- vA0", 7: "a1 apply- a0 vC0- gB2 gB1 a5 pln0- gC0 Z- a2 yr- gC1 D a3 half-- idx- eq- a4 sC scan- ga- vA0 hvo- slo- new-", 8: "vC0- pln0- half-- Z- yr- idx- store-- ga- new-", 9: "half-- store--"}
JOBS = {1: "w1", 2: "o2", 3: "w2", 4: "o3", 5: "w3"}


def bits(es):
    return sum(1 << e for e in es)


def rank_program(g, core, T, topo):
    rank = T.rank_of(core)
    if rank is None:
        return
    cores = list(T.cores)
    N = len(cores)
    Q = {"g": g, "v": g.vector, "s": g.scalar, "p": g.tensor, "y": g.sync}
    last_w, readers, totals, waited = {}, {}, {}, {}
    ndma = [0]

    def add(eng, fn, reads=(), writes=(), ext=(), kind="c"):
        need = {}
        for k in list(reads) + list(writes):
            for s, v in last_w.get(k, []) + (readers.get(k, []) if k in writes else []):
                need[s] = max(need.get(s, 0), v)
        for k in reads:
            assert k in last_w, k
        for s, v in ext:
            need[s] = max(need.get(s, 0), v)
            totals[s] = max(totals.get(s, 0), v)
        q = Q[eng]
        if eng == "p":
            need.pop("qp", None)
        for s in sorted(need):
            if waited.get((eng, s), 0) < need[s]:
                q.wait_ge(T.sem[s], int(need[s]))
                waited[(eng, s)] = need[s]
        ins = fn(q)
        if kind == "r":
            return
        if kind == "d":
            sem, step = "d%d" % ndma[0], 16
            ndma[0] += 1
        else:
            sem, step = "q" + eng, 1
        for x in ins:
            x.then_inc(T.sem[sem], step)
        totals[sem] = totals.get(sem, 0) + step * len(ins)
        for k in reads:
            readers.setdefault(k, []).append((sem, totals[sem]))
        for k in writes:
            last_w[k] = [(sem, totals[sem])]
            readers[k] = []

    def vec(fn, reads, writes, **kw):
        add("v", lambda q: [fn(q)], reads, writes, **kw)

    def act(out, in_, func, reads, writes, bias=0.0, scale=1.0, **kw):
        add("s", lambda q: [q.activation(out, in_, func, bias=bias, scale=scale)], reads, writes, **kw)

    def mm(lst, reads, writes):
        add("p", lambda q: [q.matmul(o, l, r, a, b) for o, l, r, a, b in lst], reads, writes)

    def group(lst):
        return [(o, l, r, k == 0, k == len(lst) - 1) for k, (o, l, r) in enumerate(lst)]

    def gps(fn, reads, writes):
        add("g", lambda q: [fn(q)], reads, writes)

    def dma(eng, out, in_, reads, writes, **kw):
        add(eng, lambda q: [q.dma_start(out, in_)], reads, writes, kind="d", **kw)

    def ts(out, in0, s1, s2, op0, op1=None):
        if op1 is None:
            return lambda q: q.tensor_scalar(out, in0, s1, None, op0)
        return lambda q: q.tensor_scalar(out, in0, s1, s2, op0, op1)

    def fill(out, value, keys):
        vec(lambda q: q.memset(out, value), (), keys)

    def sfill(out, value, keys):
        act(out, T.idn[:, 0:out.shape[1]], ACT.Identity, ["id%d" % k for k in range(5)], keys, scale=0.0, bias=value)

    def iota(out, pattern, base, keys):
        gps(lambda q: q.iota(out, pattern, base, 0, allow_small_or_imprecise_dtypes=True), (), keys)

    def sel(out, n, pattern, base, keys, cm=1, parts=128):
        gps(lambda q: q.affine_select(out, T.ones[0:parts, 0:n], pattern, ALU.is_equal, 0.0, base, cm), ["ones"], keys)

    def same_chip(a, b):
        return b in topo.cores_of(a)

    def far_mask(a):
        return [topo.mask(a, b) for b in cores if not same_chip(a, b)][0]

    def engines(a, b, wide=False):
        if same_chip(a, b) and wide != 1:
            return [e for e in topo.engines(a, b) if (far_mask(a) >> e & 1) == (wide == 2)]
        return list(topo.engines(a, b))

    def handed_on(r, t):
        return t >= 1 and same_chip(cores[r], cores[(r + 1) % N])

    def src_ex(r, t):
        return (r + 1) % N if handed_on(r, t) else (r + 1 + t) % N

    def src_inc(r, t):
        return src_ex(r, t) if t <= 1 else ((r + 1) % N if t < NT else (r - NT) % N)

    def src_upd(r, t):
        return (r + 1) % N if t < NT - 1 else (r - NT) % N

    def arr_ex(t):
        return ("ae%d" % t, (2 if t == 0 else 1) * len(engines(cores[src_ex(rank, t)], core, WIDE0 and t == 0)))

    def arr_inc(t):
        return ("ai%d" % t, len(engines(cores[src_inc(rank, t)], core, WIDE0 and t == 0)))

    def arr_upd(t):
        return ("au%d" % t, len(engines(cores[src_upd(rank, t)], core)))

    def send(dst, out, in_, sem, reads, ext=(), wide=False):
        es = engines(core, dst, wide)
        rid, pid = topo.addr(dst, core)
        totals["sent"] = totals.get("sent", 0) + len(es)
        add("g", lambda q: q.remote_dma(out, in_, T.sem[sem], T.sem.sent, pid, rid, bits(es)), reads, (), ext=ext, kind="r")

    def ring(t):
        return cores[(rank - 1) % N if t < NT - 1 else (rank + NT) % N]

    w2 = [T["w2_%d" % t] for t in range(NT)]
    inc = [T["inc%d" % t] for t in range(NT + 1)]
    H = C // 2
    r0, r1 = (rank - 1) % N, (rank - 2) % N

    def loads():
        what = {"s": [(w2[0][:, C:C + F], T.shp[:], ["s0_%d" % j for j in range(NB)])], "p": [(T.picw[:, HEAD:HEAD + P], T.pic[:], ["pic0"])],
                "i": [(T.inco[:], T.inc[:], ["own0"])],
                "e": [(T.exo[:, 0:H], T.ex[:, 0:H], ["own1"]), (T.exo[:, H:C], T.ex[:, H:C], ["own2"])]}
        dma("s", T.ofi[:], T.ofs[:], (), ["ofi"])
        for out, in_, keys in [x for k in LOADS for x in what[k]]:
            dma("y", out, in_, (), keys)
        dma("s", T.thi[0:8, :], T.thr[:], (), ["thi"])

    def bank0(k):
        if k == 0:
            send(cores[r0], inc[0][:, 0:C], T.inco[:], "ai0", ["own0"], wide=WIDE0)
        else:
            send(cores[r0], w2[0][:, (k - 1) * H:k * H], T.exo[:, (k - 1) * H:k * H], "ae0", ["own%d" % k], wide=WIDE0)

    def go():
        add("g", lambda q: q.sem_inc(T.sem.go, 1), kind="r")

    def copies():
        dma("y", T.picw[:, HEAD - STEP:HEAD], T.pic[:, P - STEP:P], (), ["pic2"])
        dma("y", T.picw[:, HEAD + 2 * P:HEAD + 2 * P + STEP], T.pic[:, 0:STEP], (), ["pic3"])
        dma("y", T.picw[:, HEAD + P:HEAD + 2 * P], T.pic[:], (), ["pic1_%d" % k for k in range(4)], ext=[("go", 1)])
        dma("y", T.picw[:, 0:HEAD - STEP], T.pic[:, P - HEAD:P - STEP], (), ["pic4"], ext=[("go", 1)])
        dma("y", T.picw[:, HEAD + 2 * P + STEP:PW], T.pic[:, STEP:HEAD], (), ["pic5"])

    def again(k):
        a, n = HEAD + k * P // 4, P // 4
        out, in_, key = T.picw[:, a + P:a + P + n], T.picw[:, a:a + n], ["pic1_%d" % k]
        if PICV[k] == "y":
            dma("y", out, T.pic[:, k * n:(k + 1) * n], (), key, ext=[("go", 1)] if GO else [])
        elif PICV[k] == "v":
            vec(lambda q: q.tensor_copy(out, in_), ["pic0"], key)
        else:
            act(out, in_, ACT.Copy, ["pic0"], key)

    def bank1():
        if not handed_on(r1, 1):
            send(cores[r1], inc[1][:, 0:C], T.inco[:], "ai1", ["own0"])
            send(cores[r1], w2[1][:, 0:C], T.exo[:], "ae1", ["own1", "own2"])
        if handed_on(r0, 1):
            send(cores[r0], inc[1][:, 0:C], inc[0][:, 0:C], "ai1", (), ext=[arr_inc(0)])

    def hand_on(t):
        if handed_on(r0, t):
            send(cores[r0], w2[t][:, 0:C], w2[t - 1][:, 0:C], "ae%d" % t, (), ext=[arr_ex(t - 1)], wide=0)

    def fresh(t):
        return [nm for nm in NAMES if all(SETS[t][nm] != SETS[k][nm] for k in range(t))]

    def blank(t):
        ks = [MASTERS.index(SETS[t][nm]) for nm in fresh(t)]
        (fill if t < 2 else sfill)(T.mst[:, ks[0] * MW:(ks[-1] + 1) * MW], 0.0, ["m%d" % i for i in ks] + ["mm%d" % i for i in ks])

    def masters(t):
        for nm in fresh(t):
            ms = SETS[t][nm]
            i = MASTERS.index(ms)
            o = i * MW
            if len(ms) == 2:
                sel(T.mst[:, o + 3:o + 131:4], 32, [[-16, 8], [-ms[1], 2], [-1, 2]], -ms[0], ["m%d" % i])
            else:
                for side in range(2):
                    sel(T.mst[:, o + 12 + side:o + 140:2], 64, [[-16, 8], [-1000, 4], [-ms[1], 2]], -ms[0] - ms[2] * side,
                        ["m%d" % i] if side == 0 else ["mm%d" % i])

    def master(ms, u):
        o = MASTERS.index(ms) * MW + (3 - u if len(ms) == 2 else 12 - 4 * u)
        return T.mst[:, o:o + 128]

    def mkeys(t, names):
        ks = [MASTERS.index(SETS[t][nm]) for nm in names]
        return ["m%d" % k for k in ks] + ["mm%d" % k for k in ks]

    def ident(k):
        return T.idn[:, 128 * k:128 * k + 128]

    def first():
        gps(lambda q: q.iota(T.pi[:, 0:1], [[0, 1]], 0, 1), (), ["pi"])
        fill(T.ones[:], 1.0, ["ones"])
        blank(0)
        sel(ident(0), 128, [[-1, 128]], 0, ["id0"])
        scales = [2.0 ** m for m in range(10)] + [BIG, -BIG]
        for k in (10, 11, 1, 2, 3, 4, 5, 6, 7, 8, 9):
            act(ident(k), ident(0), ACT.Copy, ["id0"], ["id%d" % k], scale=scales[k])

    def counts():
        iota(T.l2[:], [[-32, F // 16]], 0, ["l2"])
        iota(T.kr[:], [[-2, SEG]], RAW - 2 * C + 32, ["kr"])

    def fills():
        vec(ts(T.pa[:, 0:1], T.pi[:, 0:1], 15, None, ALU.bitwise_and), ["pi"], ["pa"])
        fill(T.zer[:], 0.0, ["zer"])
        vec(ts(T.af[:, 0:1], T.pa[:, 0:1], -2.0, RAW - 2.0 * C, ALU.mult, ALU.add), ["pa"], ["af"])
        for k, v in enumerate((1e6, -1e6, RAW - 2.0 * C)):
            fill(T.low[:, k:NB * 6 * B:3], v, ["low%d" % k])
        for k, v in enumerate((-2.0 ** -100, -1.0, (P - 1 - RAW / 2.0) / 4096, -1024.0)):
            fill(T.col[:, k:k + 1], v, ["col%d" % k])
        fill(T.thx[:], 0.0, ["thx"])
        fill(T.wgt[:, 6 * B * NT:6 * B * (NT + 2)], 0.0, ["wgt4"])
        fill(T.cst[:, SEG - 1:3 * SEG:SEG], 0.0, ["cst3"])
        for t in range(NT):
            fill(T["slo%d" % t][:], 0, ["slo%d" % t])

    def heads():
        sfill(T.eq[:], 2.0, ["eq%d" % k for k in range(4)])
        for t in range(NT + 1):
            sfill(inc[t][:, C:IW], 0.0, ["inc%d" % t])

    def floors():
        for j in range(NB):
            vec(ts(T.low[:, (6 * j + 3) * B + 2:(6 * j + 6) * B:3], T.l2[:, j * B:(j + 1) * B], T.af[:, 0:1], None, ALU.add), ["l2", "af", "low2"],
                ["lowb%d" % j])
        o = 3 * B + 2
        vec(ts(T.own[:, 0:3], T.low[:, o:o + 9:3], 2.0 * (P - 1 - SP + C) - RAW, 1.0 / 8192, ALU.add, ALU.mult), ["lowb0"], ["lo3"])

    def cst():
        o = 3 * B + 2
        for b in range(3):
            vec(ts(T.cst[:, b * SEG:(b + 1) * SEG - 1], T.kr[:, 0:SEG - 1], T.low[:, o + 3 * b:o + 3 * b + 1], T.own[:, b:b + 1], ALU.is_ge, ALU.max),
                ["kr", "lowb0", "lo3"], ["cst%d" % b])

    def bos():
        sel(T.bot[0:8, :], 128, [[1, 8], [0, 16]], 0, ["bot"], cm=-1, parts=8)
        mm(group([(T.pz0[:, 0:8], T.bot[0:8, :], T.idn[0:8, 0:8])]), ["bot", "id0"], ["pz0"])
        for k, a in enumerate((15 / 128, 11 / 128, 5 / 16, 1.0, 73 / 512, -7 / 64)):
            act(T.bos[:, 8 * k:8 * k + 8], T.pz0[:, 0:8], ACT.Copy, ["pz0"], ["bos%d" % k], scale=a)

    def off():
        vec(lambda q: q.tensor_copy(T.off[:], T.ofi[:]), ["ofi"], ["off"])

    def thr():
        vec(ts(T.thx[0:8, MV - MA:MV - MA + NT], T.thi[0:8, :], -2.0, 21.0, ALU.mult, ALU.add), ["thi"], ["thx"])

    def rows():
        mm(group([(T.pz0[MA:128, 0:128], T.thx[0:8, :], T.bot[0:8, :])]), ["bot", "thx"], ["pz0"])
        for j in range(NB):
            vec(lambda q: q.tensor_copy(T["pln%d" % j][MA:128, 0:128], T.pz0[MA:128, 0:128]), ["pz0"], ["pln%d" % j])

    def hot():
        for s in range(2):
            sel(T.hot[:, 8 * B * s:8 * B * (s + 1)], 8 * B, [[-2 * B, 4], [0, 2], [-2, B]], -s, ["hot%d" % s])
        sel(T.hot[:, 16 * B:20 * B], 4 * B, [[-B, 2], [0, 2], [-1, B]], -MA, ["hot2"])
        sel(T.hot[:, 20 * B:24 * B], 4 * B, [[-1, 4], [0, B]], -MV, ["hot3"])

    def hots(k, n=1):
        return T.hot[:, 2 * k * B:(2 * k + n) * B]

    def wgt(k, rows_=128):
        return T.wgt[0:rows_, 6 * B * k:6 * B * (k + 1)]

    def third(tile, o, part, k):
        return tile[:, o + 3 * B * part + k:o + 3 * B * (part + 1):3]

    def wc():
        mm(group([(T.pz1[:, 0:B], ident(10), hots(k)) for k in range(10)]) + group([(T.pz1[:, B:2 * B], ident(11 if k < 8 else 10), hots(k)) for k in range(10)]),
           ["hot0", "hot1", "hot2", "id10", "id11"], ["pz1"])

    def wd():
        for k in range(2):
            for part in range(2):
                vec(ts(third(T.wgt, 6 * B * (NT + k), part, 1), T.pz1[:, k * B:(k + 1) * B], 1.0 - 2 * part, None, ALU.mult), ["pz1", "wgt4"],
                    ["wd%d" % (2 * k + part)])

    def weights(ts_, kb):
        for t in ts_:
            o = 6 * B * (t - ts_[0])
            mm(group([(T[kb][:, o:o + 6 * B], T.zer[:, 0:128], T.zer[:, 0:6 * B])]
                     + [(T[kb][:, o + 2:o + 6 * B:3], ident(SETS[t]["m"][k]), hots(k, 2)) for k in range(10)]
                     + [(third(T[kb], o, part, 1), ident(11 - part), T.hot[:, (20 + t) * B:(21 + t) * B]) for part in range(2)]),
               ["zer", "hot0", "hot1", "hot2", "hot3"] + ["id%d" % m for m in range(12)], [kb])

    def keep_weights(ts_, kb):
        act(T.wgt[:, 6 * B * ts_[0]:6 * B * (ts_[-1] + 1)], T[kb][:, 0:6 * B * len(ts_)], ACT.Copy, [kb], ["wgt%d" % t for t in ts_], scale=-1.0)

    def ob():
        for t in range(1, NT):
            vec(ts(T.ob[:, (t - 1) * W:t * W], T.zer[:, 0:W], T.off[:, t:t + 1], None, ALU.add), ["zer", "off"], ["ob%d" % t])

    def spread(t, kb, o):
        for s, nm in enumerate(NAMES):
            mm(group([(T[kb][:, o + s * W:o + (s + 1) * W], master(SETS[t][nm], u), T.ob[:, (t - 1) * W:t * W]) for u in range(4)]),
               mkeys(t, [nm]) + ["ob%d" % t], [kb])

    def keep_spread(ts_, kb):
        vec(lambda q: q.tensor_copy(T.obl[:, 4 * W * (ts_[0] - 1):4 * W * ts_[-1]], T[kb][:, 0:4 * W * len(ts_)]), [kb], ["obl%d" % t for t in ts_])

    def io2():
        for h in range(2):
            iota(T.io2[:, h * IW // 2:(h + 1) * IW // 2], [[-2, IW // 2]], RAW - h * IW, ["io2_%d" % h])

    def prep():
        for k in range(NB + 2):
            for step, j in ((0, k), (1, k - 1), (2, k - 2)):
                sl = slice(j * FB, (j + 1) * FB)
                if not 0 <= j < NB:
                    continue
                if step == 0:
                    vec(ts(T.ta[:, sl], w2[0][:, C + j * FB:C + (j + 1) * FB], T.off[:, 0:1], None, ALU.add), ["s0_%d" % j, "off"], ["ta%d" % j])
                elif step == 1:
                    vec(ts(T.tb[:, sl], T.ta[:, sl], P - 1, None, ALU.bitwise_and), ["ta%d" % j], ["tb%d" % j])
                else:
                    vec(ts(T["xh%d" % j][:], T.tb[:, sl], -1024.0, None, ALU.add), ["tb%d" % j], ["xh%d" % j])

    def apply_update(t):
        vec(lambda q: q.tensor_copy(inc[t + 1][:, 0:IW].indirect(T["sli%d" % t][:, 0:3]), T["hvi%d" % t][:]), (), ["inc%d" % (t + 1)],
            ext=[arr_upd(t), arr_inc(t + 1)])
        if t < NT - 1:
            send(ring(t + 1), inc[t + 2][:, 0:C], inc[t + 1][:, 0:C], "ai%d" % (t + 2), ["inc%d" % (t + 1)])
        else:
            dma("s", T.yi[:], inc[NT][:, 0:C], ["inc%d" % NT], ())

    once = dict(loads=loads, first=first, counts=counts, floors=floors, cst=cst, off=off, bos=bos, fills=fills, thr=thr, rows=rows, hot=hot, wc=wc, wd=wd,
                prep=prep, ob=ob, io2=io2, go=go, copies=copies, bank1=bank1, hand1=lambda: hand_on(1), last=lambda: apply_update(NT - 1),
                heads=heads, w0=lambda: weights([0], "pd"), w0c=lambda: keep_weights([0], "pd"))
    for k in range(1, NT):
        once.update({"w%d" % k: lambda k=k: weights([k], "pw"), "w%dc" % k: lambda k=k: keep_weights([k], "pw"),
                     "o%d" % k: lambda k=k: spread(k, "pw", 0), "o%dc" % k: lambda k=k: keep_spread([k], "pw")})
    for k in range(NT):
        once["m%d" % k] = lambda k=k: masters(k)
        once["z%d" % k] = lambda k=k: blank(k)
        once["pc%d" % k] = lambda k=k: PICV[k] == "y" or again(k)
        once["b%d" % k] = lambda k=k: bank0(k)

    def batch(n):
        t, j = divmod(n, NB)
        S = SETS[t]
        pv, pd, pz, kv, kz = T["pv%d" % j], T.pd, T["pz%d" % j], "pv%d" % j, "pz%d" % j
        xh, lst, gb, gx, cmp_, cmc, pln, yr, idx, ga = (T["%s%d" % (nm, j)] for nm in ("xh", "lst", "gb", "gx", "cmp", "cmc", "pln", "yr", "idx", "ga"))
        if t == 0:
            win, pk = T.picw[:, HEAD:HEAD + P], ["pic0"]
        else:
            win = T.picw[:, HEAD - STEP * t:HEAD + 2 * P + STEP * t]
            pk = ["pic0", "pic2", "pic3"] + ["pic1_%d" % k for k in range(4)] + (["pic4", "pic5"] if t > 1 else [])
        sl = slice(j * FB, (j + 1) * FB)
        do = {}

        def lists(h, o, names, offsets):
            pl, kl, k = T["pl%d" % h], "pl%d" % h, len(names)
            picks = [(pl[:, s * W:(s + 1) * W], master(S[nm], u), xh[:, u:FB:4] if nm == "C" else xh[:, u * W:(u + 1) * W])
                     for s, nm in enumerate(names) for u in range(4)]
            if t == 0:
                if not offsets:
                    mm([x for s in range(k) for x in group(picks[4 * s:4 * s + 4])], mkeys(t, names) + ["xh%d" % j], [kl])
                return
            c0 = 4 * W * (t - 1) + o * W
            both = group([(pl[:, 0:k * W], ident(0), T.obl[:, c0:c0 + k * W])] + picks)
            if offsets:
                mm(both[:1], ["id0", "obl%d" % t], [kl])
            else:
                mm(both[1:], mkeys(t, names) + ["xh%d" % j], [kl])

        def convert(h, o, names):
            k = len(names)
            vec(ts(lst[:, o * W:(o + k) * W], T["pl%d" % h][:, 0:k * W], 1024.0 + STEP * t, None, ALU.add), ["pl%d" % h],
                ["l%s%d" % (nm, j) for nm in names])

        for h, (nm, o, names) in enumerate((("B", 0, NAMES[:1]), ("R", 1, NAMES[1:]))):
            do["O" + nm] = lambda h=h, o=o, names=names: lists(h, o, names, True)
            do["L" + nm] = lambda h=h, o=o, names=names: lists(h, o, names, False)
            do["list" + nm] = lambda h=h, o=o, names=names: convert(h, o, names)

        def pixels(nm, a, b):
            o = NAMES.index(nm) * W
            return win.indirect(lst[:, o + a:o + b])

        for h, (a, b) in enumerate(zip(BCUTS, BCUTS[1:])):
            do["gB%d" % h] = lambda a=a, b=b: act(gb[:, 16 * a:16 * b], pixels("B", a, b), ACT.Copy, pk + ["lB%d" % j],
                                                  ["gb%d_%d" % (j, k) for k in range(a // 8, b // 8)])
        for h, (a, b) in enumerate(zip(CUTS, CUTS[1:])):
            for s, op, nm in ((0, ALU.is_gt, "A1"), (1, ALU.is_lt, "A2")):
                o = MA * (a % 16) + 2 * (a // 16) + s
                dst = cmp_[:, 32 * a + s:32 * b:2] if MODE == "wl" else cmp_[:, o:o + MA * (b - a) - 2 * WL + 1:2 * WL]
                do["a%d" % (2 * h + s)] = lambda a=a, b=b, s=s, op=op, nm=nm, dst=dst: vec(
                    lambda q: q.tensor_tensor(dst, pixels(nm, a, b), gb[:, 16 * a:16 * b], op),
                    pk + ["l%s%d" % (nm, j)] + ["gb%d_%d" % (j, k) for k in range(a // 8, b // 8)],
                    ["ca%d_%d_%d" % (j, s, k) for k in range(a // 8, b // 8)])
            if n >= XP and h == WL - 1:
                keys = ["gb%d_%d" % (j, k) for k in range(a // 8, b // 8)]
                do["gX"] = lambda a=a, b=b: act(T.gs[:], pixels("A2", a, b), ACT.Copy, pk + ["lA2%d" % j], ["gs"])
                do["pX"] = lambda a=a, b=b, keys=keys: mm(group([(T.pz1[:, 0:256], ident(0), gb[:, 16 * a:16 * b])]), ["id0"] + keys, ["pz1"])
                do["a5"] = lambda a=a, b=b, dst=dst: vec(lambda q: q.tensor_tensor(dst, T.gs[:], T.pz1[:, 0:256], ALU.is_lt), ["gs", "pz1"],
                                                         ["ca%d_1_%d" % (j, k) for k in range(a // 8, b // 8)])
            if MODE == "wl":
                do["vA%d" % h] = lambda a=a, b=b: mm(
                    [(pv[32 * (w // 16):32 * (w // 16) + 32, w % 16:384:16], cmp_[:, 32 * w:32 * w + 32], T.bos[:, 0:24], True, True) for w in range(a, b)],
                    ["bos0", "bos1", "bos2"] + ["ca%d_%d_%d" % (j, s, k) for s in range(2) for k in range(a // 8, b // 8)], [kv])
        if MODE != "wl":
            do["vA0"] = lambda: mm([(pv[0:MA, a:384:16], cmp_[:, MA * a:MA * (a + 1)], T.bos[:, 0:24], True, True) for a in range(16)],
                                   ["bos0", "bos1", "bos2"] + ["ca%d_%d_%d" % (j, s, k) for s in range(2) for k in range(2 * WL)], [kv])
        for h, (a, b) in enumerate(zip(CCUTS, CCUTS[1:])):
            do["gC%d" % h] = lambda h=h, a=a, b=b: act(gx[:, 16 * a:16 * b], pixels("C", a, b), ACT.Copy, pk + ["lC%d" % j], ["gx%d_%d" % (j, h)])
        do["D"] = lambda: mm([x for pair in range(2) for x in group([(pd[:, pair * FB:(pair + 1) * FB], ident(10 + side), gx[:, 2 * pair + side:4 * FB:4])
                                                                    for side in range(2)])],
                             ["id10", "id11"] + ["gx%d_%d" % (j, h) for h in range(len(CCUTS) - 1)], ["pd"])
        do["sC"] = lambda: act(cmc[:], pd[:, 0:2 * FB], ACT.Sign, ["pd", "col0"], ["cc%d" % j], bias=T.col[:, 0:1])
        do["vC0"] = lambda: mm([(pv[MA:MV, a:384:16], cmc[:, a:2 * FB:16], T.bos[:, 24:48], True, True) for a in range(16)],
                               ["bos3", "bos4", "bos5", "cc%d" % j], [kv])
        do["pln0"] = lambda: act(pln[0:MV, :], pv[0:MV, 0:384], ACT.Sign, [kv, "col1"], ["pln%d" % j], bias=T.col[0:MV, 1:2])
        do["Z"] = lambda: mm(group([(pz[:, 0:6 * B], pln[:, 0:128], wgt(t))] +
                                   [(pz[:, 0:6 * B], pln[0:MV, 128 * k:128 * k + 128], wgt(NT - 1 + k, MV)) for k in (1, 2)]),
                             ["wgt%d" % t, "pln%d" % j] + ["wd%d" % k for k in range(4)], [kz])
        do["yr"] = lambda: vec(lambda q: q.tensor_tensor_scan(yr[:], pz[:, 0:6 * B], T.low[:, 6 * B * j:6 * B * (j + 1)], 0.0, ALU.min, ALU.max),
                               ["low0", "low1", "low2", "lowb%d" % j, kz], ["yr%d" % j])
        do["idx"] = lambda: vec(ts(idx[:], yr[:, 2:6 * B:3], -0.5, RAW / 2.0, ALU.mult, ALU.add), ["yr%d" % j], ["idx%d" % j])
        do["ga"] = lambda: act(ga[:], inc[t][:, 0:IW].indirect(idx[:, 0:B]), ACT.Identity, ["idx%d" % j, "inc%d" % t, "col3"], ["ga%d" % j],
                               bias=T.col[:, 3:4] if t < NT - 1 else 0.0, ext=[arr_inc(0)] if t == 0 else [])
        out, ko = (xh[:], "xh%d" % j) if t < NT - 1 else (T.ta[:, sl], "ta%d" % j)
        do["new"] = lambda: vec(lambda q: q.tensor_tensor(out, w2[t][:, 0:C + F].indirect(idx[:, B:2 * B]), ga[:], ALU.add),
                                ["idx%d" % j, "ga%d" % j] + ["s%d_%d" % (t, k) for k in range(NB)], [ko], ext=[arr_ex(t)])

        def store():
            vec(lambda q: q.tensor_copy(T.ysf[:, sl], T.tb[:, sl]), ["tb%d" % j], ["ysf%d" % j])
            dma("y", T.ys[:, sl], T.ysf[:, sl], ["ysf%d" % j], ())

        if t < NT - 1:
            do["half"] = lambda: vec(ts(w2[t + 1][:, C + j * FB:C + (j + 1) * FB], xh[:], 1024.0, None, ALU.add), [ko], ["s%d_%d" % (t + 1, j)])
        else:
            do["half"] = lambda: vec(ts(T.tb[:, sl], out, P - 1, None, ALU.bitwise_and), [ko], ["tb%d" % j])
            do["store"] = store
        if j:
            return do

        c0, odd = 3 * t, 3 * t % 2
        msg = T["hvo%d" % t]

        def eq():
            for b in range(3):
                act(T.eq[:, SEG * b + 16 - 16 * odd:SEG * b + 64], T.io2[:, 0:IW].indirect(idx[:, c0 - odd:c0 + 3]), ACT.Abs,
                    ["io2_0", "io2_1", "idx0", "yr0"], ["eq%d" % b], bias=yr[:, 3 * (c0 + b) + 2:3 * (c0 + b) + 3], scale=-1.0)
            act(T.eq[:, SEG - 1:3 * SEG:SEG], yr[:, 3 * c0 + 2:3 * (c0 + 3):3], ACT.Identity, ["yr0", "col2"], ["eq3"], scale=1.0 / 8192,
                bias=T.col[:, 2:3])

        def update():
            vec(ts(T["slo%d" % t][:, 0:3], T.sc[:, SEG - 1:3 * SEG:SEG], -4096.0, P - 1.0, ALU.mult, ALU.add), ["sc"], ["slo%d" % t])
            es = engines(core, ring(t))
            rid, pid = topo.addr(ring(t), core)
            h = len(es) // 2
            totals["sent"] += len(es)
            tr = [RemoteDMATransfer(dst_ids=[DstId(rid=rid, pnc=pid)], dma_engine_mask=bits(e), remote_sem=T.sem["au%d" % t], src=a, dst=b)
                  for e, a, b in ((es[:h], T["slo%d" % t][:], T["sli%d" % t][:]), (es[h:], msg[:], T["hvi%d" % t][:]))]
            add("g", lambda q: q.remote_dma_fused(tr, local_sem=T.sem.sent), ["slo%d" % t, "hvo%d" % t], (), kind="r")
            for k in range(2, NT):
                if t == 0 and not handed_on((rank - 1 - k) % N, k):
                    send(cores[(rank - 1 - k) % N], w2[k][:, 0:C], T.exo[:], "ae%d" % k, ["own1", "own2"])
            if t + 2 < NT:
                hand_on(t + 2)

        do["eq"] = eq
        do["hvo"] = lambda: vec(ts(msg[:, 0:KH], ga[:, 16 * c0:16 * c0 + KH], 0.5, 511.75 if t < NT - 1 else -0.25, ALU.mult, ALU.add),
                                ["ga0"], ["hvo%d" % t])
        do["scan"] = lambda: vec(lambda q: q.tensor_tensor_scan(T.sc[:], T.eq[:], T.cst[:], 1.0, ALU.min, ALU.max),
                                 ["eq%d" % k for k in range(4)] + ["cst%d" % k for k in range(4)], ["sc"])
        do["slo"] = update
        if t:
            do["apply"] = lambda: apply_update(t - 1)
        return do

    batches = [batch(n) for n in range(NT * NB)]

    def run(order, n):
        for name in order.split():
            m = n + name.count("+") - name.count("-")
            nm = name.rstrip("+-")
            if nm[:3] == "job":
                nm = JOBS[m] + nm[3:] if m in JOBS else ""
            if nm in once:
                once.pop(nm)()
            elif 0 <= m < len(batches) and nm in batches[m]:
                batches[m].pop(nm)()

    run(START, 0)
    for n in range(-2, NT * NB + 3):
        run(OTHER.get(n, SLOT), n)
    run("last", 0)
    for s in sorted(totals):
        if max([v for (e, k), v in waited.items() if k == s] + [0]) < totals[s]:
            g.wait_ge(T.sem[s], int(totals[s]))
